import numpy as np
import ml_dtypes


def mxq(x, axis, fmt="e4m3"):
    dtype, down = {"e4m3": (ml_dtypes.float8_e4m3fn, 7), "e5m2": (ml_dtypes.float8_e5m2, 14)}[fmt]
    v = np.moveaxis(np.asarray(x, np.float32).astype(ml_dtypes.bfloat16).astype(np.float64), axis, -1)
    blocks = v.reshape(v.shape[:-1] + (-1, 32))
    amax = np.abs(blocks).max(-1, keepdims=True)
    byte = np.maximum(np.where(amax > 0, np.frexp(amax)[1] - 1 + 127, 0) - down, 1)
    scale = np.exp2(byte - 127.0)
    codes = (blocks / scale).astype(np.float32).astype(dtype).astype(np.float64)
    return np.moveaxis((codes * scale).reshape(v.shape), -1, axis)


WIDE = False


def mx_kscale(k):
    if not WIDE:
        return np.ones(k)
    levels = np.array([10, -10, 5, -5, 0])
    if k % 512:
        return np.exp2(np.random.permutation(np.resize(levels, k // 32))).repeat(32)
    a = np.empty((k // 512, 16))
    for p in range(k // 512):
        a[p, :8] = np.random.permutation(np.resize(levels, 8))
        for g in range(8):
            far = levels[np.abs(levels - a[p, g]) >= 10]
            a[p, g + 8] = far[np.random.randint(len(far))]
    return np.exp2(a.ravel()).repeat(32)


def f64(x):
    return np.asarray(x).astype(np.float64)


def striped(idx):
    return np.tile(idx.reshape(-1, 16).T, (8, 1)).astype(np.uint16)


def unstriped(offs):
    return offs[:16].T.reshape(-1).astype(np.int64)


E2M1 = np.array([0.0, 0.5, 1.0, 1.5, 2.0, 3.0, 4.0, 6.0, -0.0, -0.5, -1.0, -1.5, -2.0, -3.0, -4.0, -6.0])


def pack_weight(w, fmt):
    k, n = w.shape
    w = f64(np.asarray(w, np.float32).astype(ml_dtypes.bfloat16)).reshape(k // 32, 32, n)
    amax = np.abs(w).max(1)
    if fmt == "e4m3":
        byte = np.frexp(amax)[1] - 1 + 127 - 7
    else:
        mant, ex = np.frexp(amax / 6.0)
        byte = np.where(mant > 0.5, ex, ex - 1) + 127
    byte = np.clip(np.where(amax > 0, byte, 1), 1, 254)
    scaled = (w * np.exp2(127.0 - byte)[:, None, :]).reshape(k, n).astype(np.float32)
    by_word = np.ascontiguousarray(scaled.reshape(k // 512, 128, 4, n).transpose(0, 1, 3, 2))
    if fmt == "e4m3":
        words = by_word.astype(ml_dtypes.float8_e4m3fn).view(np.uint8)
    else:
        c = by_word.astype(ml_dtypes.float4_e2m1fn).view(np.uint8) & 0xF
        words = (c[..., 0::2] | (c[..., 1::2] << 4)).reshape(k // 512, 128, 2 * n)
    return np.ascontiguousarray(words), np.ascontiguousarray(byte.astype(np.uint8).reshape(k // 512, 16, n))


def unpack_weight(words, scales, fmt):
    g, _, n = scales.shape
    words = np.ascontiguousarray(words).reshape(g, 128, n, -1)
    if fmt == "e4m3":
        vals = words.view(ml_dtypes.float8_e4m3fn).astype(np.float64)
    else:
        nib = np.empty((g, 128, n, 4), np.uint8)
        nib[..., 0::2] = words & 0xF
        nib[..., 1::2] = words >> 4
        vals = E2M1[nib]
    vals = vals * np.repeat(np.exp2(scales.astype(np.float64) - 127.0), 8, axis=1)[..., None]
    return vals.transpose(0, 1, 3, 2).reshape(g * 512, n)


def gelu(v):
    return 0.5 * v * (1.0 + np.tanh(np.sqrt(2.0 / np.pi) * (v + 0.044715 * v**3)))


K, T, S, H, N = 1024, 4096, 1024, 512, 512


def setup_inputs():
    n = np.random.standard_normal
    s, u = mx_kscale(K)[:, None], mx_kscale(H)[:, None]
    tab_words, tab_scales = pack_weight(n((K, T)) * s, "e4m3")
    wb_words, wb_scales = pack_weight(n((K, H)) / np.sqrt(K) / s, "e2m1")
    wc_words, wc_scales = pack_weight(n((K, H)) / np.sqrt(K) / s * u.T, "e4m3")
    return {
        "tab_words": tab_words, "tab_scales": tab_scales,
        "offs": striped(np.random.permutation(T)[:S]),
        "wa": (n((K, H)) / np.sqrt(K) / s * u.T).astype(np.float32),
        "wb_words": wb_words, "wb_scales": wb_scales,
        "wc_words": wc_words, "wc_scales": wc_scales,
        "bb": (0.5 * n(H)).astype(np.float32),
        "wf": (n((H, N)) / np.sqrt(H) / u).astype(np.float32),
        "bf": (0.5 * n(N)).astype(np.float32),
    }


def reference(tab_words, tab_scales, offs, wa, wb_words, wb_scales, wc_words, wc_scales, bb, wf, bf):
    v = unpack_weight(tab_words, tab_scales, "e4m3")[:, unstriped(offs)]
    wb = unpack_weight(wb_words, wb_scales, "e2m1")
    wc = unpack_weight(wc_words, wc_scales, "e4m3")
    a = mxq(f64(wa), 0, "e4m3").T @ v
    b = (wb.T @ v) + f64(bb)[:, None]
    c = wc.T @ v
    h = a * b + c
    y = mxq(f64(wf), 0, "e4m3").T @ mxq(h, 0, "e4m3")
    return y + f64(bf)[:, None]

@@ -1,0 +1,317 @@
+from contextlib import ExitStack
+
+import concourse.mybir as mybir
+
+K, T, S, H, N = 1024, 4096, 1024, 512, 512
+FLOPS = 2 * S * (3 * K * H + H * N)
+
+F32 = mybir.dt.float32
+BF16 = mybir.dt.bfloat16
+I32 = mybir.dt.int32
+U32 = mybir.dt.uint32
+U16 = mybir.dt.uint16
+U8 = mybir.dt.uint8
+FP8X4 = mybir.dt.float8_e4m3fn_x4
+FP4X4 = mybir.dt.float4_e2m1fn_x4
+ADD = mybir.AluOpType.add
+MULT = mybir.AluOpType.mult
+IDENTITY = mybir.ActivationFunctionType.Identity
+
+P = 128
+HALF = 512
+
+
+def tile_list_bilinear_flux_update_kernel(
+    tc, tab_words, tab_scales, offs, wa, wb_words, wb_scales, wc_words, wc_scales, bb, wf, bf, out
+):
+    nc = tc.nc
+    with ExitStack() as ctx:
+        lists = ctx.enter_context(tc.tile_pool(name="lists", bufs=1))
+        sb = ctx.enter_context(tc.tile_pool(name="sb", bufs=1))
+        shared = ctx.enter_context(tc.tile_pool(name="shared", bufs=1))
+        psum = ctx.enter_context(tc.psum_pool(name="psum", bufs=1))
+
+        def tile(name, shape, dtype):
+            return sb.tile(shape, dtype, name=name, align_bytes=64)
+
+        def placed(name, shape, dtype, kib):
+            return shared.tile(shape, dtype, name=name, align_bytes=64, offset=1024 * kib)
+
+        bank = [psum.tile([P, 512], F32, name=f"bank{i}") for i in range(8)]
+
+        offsets = lists.tile([P, S // 16], U16, name="offsets")
+        table = [placed(f"table{a}", [P, T], U32, 16 * a) for a in range(2)]
+        table_sc = placed("table_sc", [P, T], U8, 37)
+        w_sc_raw = tile("w_sc_raw", [P, 2, 2, H], U8)
+        v_sc = tile("v_sc", [P, S], U8)
+        v_sc1 = tile("v_sc1", [P, S], U8)
+        wb_raw = tile("wb_raw", [P, 2, 2 * H], U8)
+        wc_raw = tile("wc_raw", [P, 2, H], I32)
+        bb_col = tile("bb_col", [P, 4], F32)
+        bf_col = tile("bf_col", [P, 4], F32)
+
+        nc.vector.memset(table_sc[:].bitcast(I32), 0)
+        nc.vector.memset(w_sc_raw[:].rearrange("p w a n -> p (w a n)").bitcast(I32), 0)
+        nc.vector.memset(v_sc1[:].bitcast(I32), 0)
+
+        def load_words(a):
+            words = tab_words[a].rearrange("p t i -> p (t i)").bitcast(I32)
+            for s in range(2):
+                cols = slice(s * T // 2, (s + 1) * T // 2)
+                nc.sync.dma_start(out=table[a][:, cols].bitcast(I32), in_=words[:, cols])
+
+        def load_w_scales(engine, w, src, row0):
+            for q in range(4):
+                engine.dma_start(
+                    out=w_sc_raw[32 * q + row0 : 32 * q + row0 + 4, w, :, :].bitcast(I32),
+                    in_=src[:, 4 * q : 4 * q + 4, :].rearrange("a r n -> r a n").bitcast(I32),
+                )
+
+        nc.sync.dma_start(offsets[:], offs)
+        nc.sync.dma_start(out=wb_raw[:].bitcast(I32), in_=wb_words.rearrange("a p n -> p a n").bitcast(I32))
+        load_words(0)
+        for q in range(4):
+            nc.sync.dma_start(
+                out=table_sc[32 * q : 32 * q + 8, :].bitcast(I32),
+                in_=tab_scales[:, 4 * q : 4 * q + 4, :].bitcast(I32),
+            )
+        load_words(1)
+        nc.sync.dma_start(out=wc_raw[:], in_=wc_words.rearrange("a p n i -> p a (n i)").bitcast(I32))
+
+        with nc.allow_non_contiguous_dma(reason="one bias value a partition"):
+            bb_rows = bb.rearrange("(u j e) -> e u j", j=4, e=4)
+            for e in range(4):
+                nc.scalar.dma_start(out=bb_col[e:P:4, :], in_=bb_rows[e])
+            load_w_scales(nc.scalar, 0, wb_scales, 0)
+            load_w_scales(nc.gpsimd, 1, wc_scales, 4)
+            nc.gpsimd.dma_start(out=bf_col[:], in_=bf.rearrange("(t p) -> p t", p=P))
+
+        v = [
+            [tile("v00", [P, HALF], U32), placed("v01", [P, HALF], U32, 37)],
+            [tile("v10", [P, HALF], U32), tile("v11", [P, HALF], U32)],
+        ]
+
+        def gather_words(a, h):
+            nc.vector.tensor_copy(v[a][h][:], table[a][:].indirect(offsets[:, 32 * h : 32 * (h + 1)]))
+
+        def v_plane(a, cols):
+            return v_sc[4 * a : P, cols]
+
+        nc.vector.tensor_copy(v_sc[:], table_sc[:].indirect(offsets[:]))
+        for q in range(4):
+            nc.scalar.dma_start(
+                out=v_sc1[32 * q : 32 * q + 4, :].bitcast(I32), in_=v_sc[32 * q + 4 : 32 * q + 8, :].bitcast(I32)
+            )
+
+        wb_q = tile("wb_q", [P, 2, 2 * H], U8)
+        wc_q = placed("wc_q", [P, 2, H], U32, 16)
+        w_sc = [tile("wb_sc", [P, 2, H], U8), placed("wc_sc", [P, 2, H], U8, 28)]
+
+        def permute_scales(w):
+            nc.vector.tensor_copy(
+                w_sc[w][:].bitcast(I32).rearrange("p a (t u) -> p a t u", t=4),
+                w_sc_raw[:, w, :, :].bitcast(I32).rearrange("p a (u t) -> p a t u", t=4),
+            )
+
+        gather_words(0, 0)
+        nc.vector.tensor_copy(
+            wb_q[:].bitcast(I32).rearrange("p a (t u e) -> p a t u e", t=4, e=2),
+            wb_raw[:].bitcast(I32).rearrange("p a (u t e) -> p a t u e", t=4, e=2),
+        )
+        permute_scales(0)
+        gather_words(0, 1)
+
+        wa_raw = [[placed(f"wa_raw{a}{s}", [P, 4, H // 2], F32, 8 * a + 4 * s) for s in range(2)] for a in range(2)]
+        wa_rows = wa.rearrange("(a p j) c -> a p j c", a=2, j=4)
+        for a in range(2):
+            for s in range(2):
+                nc.sync.dma_start(out=wa_raw[a][s][:], in_=wa_rows[a][:, :, s * 256 : (s + 1) * 256])
+
+        def b_pass(a, h, j):
+            cols = slice(h * HALF, (h + 1) * HALF)
+            nc.tensor.matmul_mx(
+                out=bank[4 * h + j][:],
+                lhsT=wb_q[:, a, 256 * j : 256 * (j + 1)].bitcast(FP4X4),
+                lhsT_scale=w_sc[0][:, a, 128 * j : 128 * (j + 1)],
+                rhs=v[a][h][:].bitcast(FP8X4),
+                rhs_scale=(v_sc, v_sc1)[a][:, cols],
+                start=(a == 0),
+                stop=(a == 1),
+            )
+
+        for h in range(2):
+            for j in range(4):
+                b_pass(0, h, j)
+
+        b_sb = [tile(f"b_sb{h}", [P, 4, HALF], F32) for h in range(2)]
+        for h in range(2):
+            gather_words(1, h)
+            for j in range(4):
+                b_pass(1, h, j)
+                nc.scalar.activation(b_sb[h][:, j, :], bank[4 * h + j][:], IDENTITY, bias=bb_col[:, j : j + 1])
+
+        wf_raw = placed("wf_raw", [P, 4, N], F32, 29)
+        wf_rows = wf.rearrange("(u j e) n -> e u j n", j=4, e=4)
+        for e in range(4):
+            nc.sync.dma_start(out=wf_raw[e:P:4, :, :], in_=wf_rows[e])
+
+        nc.vector.tensor_copy(
+            wc_q[:].bitcast(I32).rearrange("p a (t u e) -> p a t u e", t=4, e=4),
+            wc_raw[:].rearrange("p a (u t e) -> p a t u e", t=4, e=4),
+        )
+        permute_scales(1)
+
+        def c_group(g):
+            h, n0 = divmod(128 * g, HALF)
+            for j in range(4):
+                for a in range(2):
+                    nc.tensor.matmul_mx(
+                        out=bank[g % 4][:, 128 * j : 128 * (j + 1)],
+                        lhsT=wc_q[:, a, 128 * j : 128 * (j + 1)].bitcast(FP8X4),
+                        lhsT_scale=w_sc[1][4:P, a, 128 * j : 128 * (j + 1)],
+                        rhs=v[a][h][:, n0 : n0 + 128].bitcast(FP8X4),
+                        rhs_scale=v_plane(a, slice(128 * g, 128 * (g + 1))),
+                        start=(a == 0),
+                        stop=(a == 1),
+                    )
+
+        for g in range(4):
+            c_group(g)
+
+        wa_bf = [placed(f"wa_bf{a}", [P, 4 * H], BF16, 20 + 4 * a) for a in range(2)]
+        wa_q = [tile(f"wa_q{a}", [P, H], U32) for a in range(2)]
+        wa_sc = [tile(f"wa_sc{a}", [P, H], U8) for a in range(2)]
+
+        def a_pass(dst, a, j, n0, n):
+            h, m0 = divmod(n0, HALF)
+            nc.tensor.matmul_mx(
+                out=dst,
+                lhsT=wa_q[a][:, 128 * j : 128 * (j + 1)].bitcast(FP8X4),
+                lhsT_scale=wa_sc[a][:, 128 * j : 128 * (j + 1)],
+                rhs=v[a][h][:, m0 : m0 + n].bitcast(FP8X4),
+                rhs_scale=v_plane(a, slice(n0, n0 + n)),
+                start=(a == 0),
+                stop=(a == 1),
+            )
+
+        wa_dst = [wa_bf[a][:].rearrange("p (t s u e j) -> p s t u j e", t=4, s=2, e=4, j=4) for a in range(2)]
+        wa_src = [
+            [wa_raw[a][s][:].rearrange("p j (u t e) -> p t u j e", t=4, e=4) for s in range(2)] for a in range(2)
+        ]
+        for s in range(2):
+            nc.vector.tensor_copy(wa_dst[0][:, s], wa_src[0][s])
+        nc.vector.quantize_mx(out=wa_q[0][:].bitcast(FP8X4), scales=wa_sc[0][:], in_=wa_bf[0][:])
+        for j in range(4):
+            a_pass(bank[4 + j][:], 0, j, 0, HALF)
+
+        nc.vector.tensor_copy(wa_dst[1][:, 0], wa_src[1][0])
+        for t in range(2):
+            nc.vector.tensor_copy(wa_dst[1][:, 1, t], wa_src[1][1][:, t])
+        for t in range(2, 4):
+            nc.scalar.copy(wa_dst[1][:, 1, t], wa_src[1][1][:, t])
+        for j in range(4):
+            nc.vector.quantize_mx(
+                out=wa_q[1][:, 128 * j : 128 * (j + 1)].bitcast(FP8X4),
+                scales=wa_sc[1][:, 128 * j : 128 * (j + 1)],
+                in_=wa_bf[1][:, 512 * j : 512 * (j + 1)],
+            )
+            a_pass(bank[4 + j][:], 1, j, 0, HALF)
+
+        ab = [tile("ab0", [P, 4, HALF], F32), placed("ab1", [P, 4, HALF], F32, 29)]
+        for j in range(4):
+            nc.vector.tensor_tensor(ab[0][:, j, :], bank[4 + j][:], b_sb[0][:, j, :], MULT)
+
+        wf_bf = placed("wf_bf", [P, 4 * N], BF16, 41)
+        wf_q = tile("wf_q", [P, N], U32)
+        wf_sc = tile("wf_sc", [P, N], U8)
+        wf_dst = wf_bf[:].rearrange("p (c i j) -> p c j i", i=4, j=4)
+        wf_src = wf_raw[:].rearrange("p j (c i) -> p c j i", i=4)
+        for s in range(2):
+            nc.scalar.copy(wf_dst[:, 64 * s : 64 * (s + 1)], wf_src[:, 64 * s : 64 * (s + 1)])
+
+        h_bf = [
+            placed("h_bf1", [P, 1024], BF16, 41) if c == 1 else tile(f"h_bf{c}", [P, 1024], BF16) for c in range(4)
+        ]
+        h_q = tile("h_q", [P, S], U32)
+        h_sc = tile("h_sc", [P, S], U8)
+        out_rows = out.rearrange("(t p) s -> p t s", p=P)
+
+        def finish_h(g):
+            h, n0 = divmod(128 * g, HALF)
+            nc.vector.tensor_tensor(
+                h_bf[g // 2][:, 512 * (g % 2) : 512 * (g % 2 + 1)].rearrange("p (c i j) -> p c j i", i=2, j=4),
+                bank[g % 4][:].rearrange("p (j c i) -> p c j i", j=4, i=2),
+                ab[h][:, :, n0 : n0 + 128].rearrange("p j (c i) -> p c j i", i=2),
+                ADD,
+            )
+            if g < 4:
+                c_group(g + 4)
+
+        def quantize_h(n0, n):
+            nc.vector.quantize_mx(
+                out=h_q[:, n0 : n0 + n].bitcast(FP8X4),
+                scales=h_sc[:, n0 : n0 + n],
+                in_=h_bf[n0 // 256][:, 4 * (n0 % 256) : 4 * (n0 % 256 + n)],
+            )
+
+        def flux(n0, n, banks, vector_share):
+            y = tile(f"y{n0}", [P, 4, n], F32)
+            for t in range(4):
+                nc.tensor.matmul_mx(
+                    out=bank[banks[t // 2]][:, (t % 2) * n : (t % 2 + 1) * n],
+                    lhsT=wf_q[:, 128 * t : 128 * (t + 1)].bitcast(FP8X4),
+                    lhsT_scale=wf_sc[:, 128 * t : 128 * (t + 1)],
+                    rhs=h_q[:, n0 : n0 + n].bitcast(FP8X4),
+                    rhs_scale=h_sc[:, n0 : n0 + n],
+                    start=True,
+                    stop=True,
+                )
+            for t in range(4):
+                src = bank[banks[t // 2]][:, (t % 2) * n : (t % 2 + 1) * n]
+                if t in vector_share:
+                    nc.vector.tensor_scalar(y[:, t, :], src, bf_col[:, t : t + 1], None, ADD)
+                else:
+                    nc.scalar.activation(y[:, t, :], src, IDENTITY, bias=bf_col[:, t : t + 1])
+            nc.sync.dma_start(out=out_rows[:, :, n0 : n0 + n], in_=y[:])
+
+        def a_pair(n0, jj):
+            for j in (2 * jj, 2 * jj + 1):
+                for a in range(2):
+                    a_pass(bank[4 + jj][:, (j % 2) * 256 : (j % 2 + 1) * 256], a, j, n0, 256)
+
+        def multiply_pair(n0, jj):
+            cols = slice(n0 - HALF, n0 - HALF + 256)
+            nc.vector.tensor_tensor(
+                ab[1][:, 2 * jj : 2 * jj + 2, cols],
+                bank[4 + jj][:].rearrange("p (j n) -> p j n", j=2),
+                b_sb[1][:, 2 * jj : 2 * jj + 2, cols],
+                MULT,
+            )
+
+        a_pair(512, 0)
+        a_pair(512, 1)
+        finish_h(0)
+        finish_h(1)
+        nc.vector.quantize_mx(out=wf_q[:].bitcast(FP8X4), scales=wf_sc[:], in_=wf_bf[:])
+        finish_h(2)
+        quantize_h(0, 256)
+        flux(0, 256, (6, 7), ())
+        finish_h(3)
+        multiply_pair(512, 0)
+        a_pair(768, 0)
+        quantize_h(256, 256)
+        flux(256, 256, (6, 7), ())
+        multiply_pair(512, 1)
+        a_pair(768, 1)
+        multiply_pair(768, 0)
+        finish_h(4)
+        finish_h(5)
+        multiply_pair(768, 1)
+        quantize_h(512, 256)
+        flux(512, 256, (6, 7), ())
+        finish_h(6)
+        finish_h(7)
+        quantize_h(768, 128)
+        flux(768, 128, (0, 1), ())
+        quantize_h(896, 128)
+        flux(896, 128, (4, 5), (2, 3))

@@ -42,7 +42,8 @@ def tile_list_bilinear_flux_update_kernel(
         offsets = lists.tile([P, S // 16], U16, name="offsets")
         table = [placed(f"table{a}", [P, T], U32, 16 * a) for a in range(2)]
         table_sc = placed("table_sc", [P, T], U8, 37)
-        w_sc_raw = tile("w_sc_raw", [P, 2, 2, H], U8)
+        wb_sc_raw = placed("wb_sc_raw", [P, 2, H], U8, 41)
+        wc_sc_raw = tile("wc_sc_raw", [P, 2, H], U8)
         v_sc = tile("v_sc", [P, S], U8)
         v_sc1 = tile("v_sc1", [P, S], U8)
         wb_raw = tile("wb_raw", [P, 2, 2 * H], U8)
@@ -51,43 +52,44 @@ def tile_list_bilinear_flux_update_kernel(
         bf_col = tile("bf_col", [P, 4], F32)
 
         nc.vector.memset(table_sc[:].bitcast(I32), 0)
-        nc.vector.memset(w_sc_raw[:].rearrange("p w a n -> p (w a n)").bitcast(I32), 0)
+        nc.vector.memset(wb_sc_raw[:].bitcast(I32), 0)
+        nc.vector.memset(wc_sc_raw[:].bitcast(I32), 0)
         nc.vector.memset(v_sc1[:].bitcast(I32), 0)
 
-        def load_words(a):
+        def load_words(a, cols):
             words = tab_words[a].rearrange("p t i -> p (t i)").bitcast(I32)
-            for s in range(2):
-                cols = slice(s * T // 2, (s + 1) * T // 2)
-                nc.sync.dma_start(out=table[a][:, cols].bitcast(I32), in_=words[:, cols])
+            nc.sync.dma_start(out=table[a][:, cols].bitcast(I32), in_=words[:, cols])
 
-        def load_w_scales(engine, w, src, row0):
+        def load_w_scales(engine, dst, src, row0):
             for q in range(4):
                 engine.dma_start(
-                    out=w_sc_raw[32 * q + row0 : 32 * q + row0 + 4, w, :, :].bitcast(I32),
+                    out=dst[32 * q + row0 : 32 * q + row0 + 4, :, :].bitcast(I32),
                     in_=src[:, 4 * q : 4 * q + 4, :].rearrange("a r n -> r a n").bitcast(I32),
                 )
 
         nc.sync.dma_start(offsets[:], offs)
+        load_words(0, slice(0, 2048))
         nc.sync.dma_start(out=wb_raw[:].bitcast(I32), in_=wb_words.rearrange("a p n -> p a n").bitcast(I32))
-        load_words(0)
         for q in range(4):
             nc.sync.dma_start(
                 out=table_sc[32 * q : 32 * q + 8, :].bitcast(I32),
                 in_=tab_scales[:, 4 * q : 4 * q + 4, :].bitcast(I32),
             )
-        load_words(1)
+        load_words(0, slice(2048, T))
+        load_w_scales(nc.sync, wb_sc_raw, wb_scales, 0)
+        load_words(1, slice(0, 2560))
+        load_w_scales(nc.sync, wc_sc_raw, wc_scales, 4)
+        load_words(1, slice(2560, T))
         nc.sync.dma_start(out=wc_raw[:], in_=wc_words.rearrange("a p n i -> p a (n i)").bitcast(I32))
 
         with nc.allow_non_contiguous_dma(reason="one bias value a partition"):
             bb_rows = bb.rearrange("(u j e) -> e u j", j=4, e=4)
             for e in range(4):
-                nc.scalar.dma_start(out=bb_col[e:P:4, :], in_=bb_rows[e])
-            load_w_scales(nc.scalar, 0, wb_scales, 0)
-            load_w_scales(nc.gpsimd, 1, wc_scales, 4)
+                nc.gpsimd.dma_start(out=bb_col[e:P:4, :], in_=bb_rows[e])
             nc.gpsimd.dma_start(out=bf_col[:], in_=bf.rearrange("(t p) -> p t", p=P))
 
         v = [
-            [tile("v00", [P, HALF], U32), placed("v01", [P, HALF], U32, 37)],
+            [tile("v00", [P, HALF], U32), placed("v01", [P, HALF], U32, 41)],
             [tile("v10", [P, HALF], U32), tile("v11", [P, HALF], U32)],
         ]
 
@@ -99,7 +101,7 @@ def tile_list_bilinear_flux_update_kernel(
 
         nc.vector.tensor_copy(v_sc[:], table_sc[:].indirect(offsets[:]))
         for q in range(4):
-            nc.scalar.dma_start(
+            nc.sync.dma_start(
                 out=v_sc1[32 * q : 32 * q + 4, :].bitcast(I32), in_=v_sc[32 * q + 4 : 32 * q + 8, :].bitcast(I32)
             )
 
@@ -110,7 +112,7 @@ def tile_list_bilinear_flux_update_kernel(
         def permute_scales(w):
             nc.vector.tensor_copy(
                 w_sc[w][:].bitcast(I32).rearrange("p a (t u) -> p a t u", t=4),
-                w_sc_raw[:, w, :, :].bitcast(I32).rearrange("p a (u t) -> p a t u", t=4),
+                (wb_sc_raw, wc_sc_raw)[w][:].bitcast(I32).rearrange("p a (u t) -> p a t u", t=4),
             )
 
         gather_words(0, 0)
@@ -121,11 +123,10 @@ def tile_list_bilinear_flux_update_kernel(
         permute_scales(0)
         gather_words(0, 1)
 
-        wa_raw = [[placed(f"wa_raw{a}{s}", [P, 4, H // 2], F32, 8 * a + 4 * s) for s in range(2)] for a in range(2)]
+        wa_raw = [placed(f"wa_raw{a}", [P, 4, H], F32, 8 * a) for a in range(2)]
         wa_rows = wa.rearrange("(a p j) c -> a p j c", a=2, j=4)
         for a in range(2):
-            for s in range(2):
-                nc.sync.dma_start(out=wa_raw[a][s][:], in_=wa_rows[a][:, :, s * 256 : (s + 1) * 256])
+            nc.sync.dma_start(out=wa_raw[a][:], in_=wa_rows[a])
 
         def b_pass(a, h, j):
             cols = slice(h * HALF, (h + 1) * HALF)
@@ -166,7 +167,7 @@ def tile_list_bilinear_flux_update_kernel(
             for j in range(4):
                 for a in range(2):
                     nc.tensor.matmul_mx(
-                        out=bank[g % 4][:, 128 * j : 128 * (j + 1)],
+                        out=bank[4 + g % 4][:, 128 * j : 128 * (j + 1)],
                         lhsT=wc_q[:, a, 128 * j : 128 * (j + 1)].bitcast(FP8X4),
                         lhsT_scale=w_sc[1][4:P, a, 128 * j : 128 * (j + 1)],
                         rhs=v[a][h][:, n0 : n0 + 128].bitcast(FP8X4),
@@ -194,34 +195,30 @@ def tile_list_bilinear_flux_update_kernel(
                 stop=(a == 1),
             )
 
-        wa_dst = [wa_bf[a][:].rearrange("p (t s u e j) -> p s t u j e", t=4, s=2, e=4, j=4) for a in range(2)]
-        wa_src = [
-            [wa_raw[a][s][:].rearrange("p j (u t e) -> p t u j e", t=4, e=4) for s in range(2)] for a in range(2)
-        ]
-        for s in range(2):
-            nc.vector.tensor_copy(wa_dst[0][:, s], wa_src[0][s])
+        wa_dst = [wa_bf[a][:].rearrange("p (t u e j) -> p t u j e", t=4, e=4, j=4) for a in range(2)]
+        wa_src = [wa_raw[a][:].rearrange("p j (u t e) -> p t u j e", t=4, e=4) for a in range(2)]
+        nc.vector.tensor_copy(wa_dst[0], wa_src[0])
         nc.vector.quantize_mx(out=wa_q[0][:].bitcast(FP8X4), scales=wa_sc[0][:], in_=wa_bf[0][:])
         for j in range(4):
-            a_pass(bank[4 + j][:], 0, j, 0, HALF)
+            a_pass(bank[j][:], 0, j, 0, HALF)
 
-        nc.vector.tensor_copy(wa_dst[1][:, 0], wa_src[1][0])
         for t in range(2):
-            nc.vector.tensor_copy(wa_dst[1][:, 1, t], wa_src[1][1][:, t])
+            nc.vector.tensor_copy(wa_dst[1][:, t], wa_src[1][:, t])
         for t in range(2, 4):
-            nc.scalar.copy(wa_dst[1][:, 1, t], wa_src[1][1][:, t])
+            nc.scalar.copy(wa_dst[1][:, t], wa_src[1][:, t])
         for j in range(4):
             nc.vector.quantize_mx(
                 out=wa_q[1][:, 128 * j : 128 * (j + 1)].bitcast(FP8X4),
                 scales=wa_sc[1][:, 128 * j : 128 * (j + 1)],
                 in_=wa_bf[1][:, 512 * j : 512 * (j + 1)],
             )
-            a_pass(bank[4 + j][:], 1, j, 0, HALF)
+            a_pass(bank[j][:], 1, j, 0, HALF)
 
         ab = [tile("ab0", [P, 4, HALF], F32), placed("ab1", [P, 4, HALF], F32, 29)]
-        for j in range(4):
-            nc.vector.tensor_tensor(ab[0][:, j, :], bank[4 + j][:], b_sb[0][:, j, :], MULT)
+        for j, cols in ((0, slice(0, 512)), (1, slice(0, 512)), (2, slice(0, 512)), (3, slice(0, 256)), (3, slice(256, 512))):
+            nc.vector.tensor_tensor(ab[0][:, j, cols], bank[j][:, cols], b_sb[0][:, j, cols], MULT)
 
-        wf_bf = placed("wf_bf", [P, 4 * N], BF16, 41)
+        wf_bf = placed("wf_bf", [P, 4 * N], BF16, 43)
         wf_q = tile("wf_q", [P, N], U32)
         wf_sc = tile("wf_sc", [P, N], U8)
         wf_dst = wf_bf[:].rearrange("p (c i j) -> p c j i", i=4, j=4)
@@ -230,7 +227,7 @@ def tile_list_bilinear_flux_update_kernel(
             nc.scalar.copy(wf_dst[:, 64 * s : 64 * (s + 1)], wf_src[:, 64 * s : 64 * (s + 1)])
 
         h_bf = [
-            placed("h_bf1", [P, 1024], BF16, 41) if c == 1 else tile(f"h_bf{c}", [P, 1024], BF16) for c in range(4)
+            placed("h_bf1", [P, 1024], BF16, 43) if c == 1 else tile(f"h_bf{c}", [P, 1024], BF16) for c in range(4)
         ]
         h_q = tile("h_q", [P, S], U32)
         h_sc = tile("h_sc", [P, S], U8)
@@ -240,12 +237,10 @@ def tile_list_bilinear_flux_update_kernel(
             h, n0 = divmod(128 * g, HALF)
             nc.vector.tensor_tensor(
                 h_bf[g // 2][:, 512 * (g % 2) : 512 * (g % 2 + 1)].rearrange("p (c i j) -> p c j i", i=2, j=4),
-                bank[g % 4][:].rearrange("p (j c i) -> p c j i", j=4, i=2),
+                bank[4 + g % 4][:].rearrange("p (j c i) -> p c j i", j=4, i=2),
                 ab[h][:, :, n0 : n0 + 128].rearrange("p j (c i) -> p c j i", i=2),
                 ADD,
             )
-            if g < 4:
-                c_group(g + 4)
 
         def quantize_h(n0, n):
             nc.vector.quantize_mx(
@@ -254,64 +249,84 @@ def tile_list_bilinear_flux_update_kernel(
                 in_=h_bf[n0 // 256][:, 4 * (n0 % 256) : 4 * (n0 % 256 + n)],
             )
 
+        def flux_pass(dst, t, n0, n):
+            nc.tensor.matmul_mx(
+                out=dst,
+                lhsT=wf_q[:, 128 * t : 128 * (t + 1)].bitcast(FP8X4),
+                lhsT_scale=wf_sc[:, 128 * t : 128 * (t + 1)],
+                rhs=h_q[:, n0 : n0 + n].bitcast(FP8X4),
+                rhs_scale=h_sc[:, n0 : n0 + n],
+                start=True,
+                stop=True,
+            )
+
+        def add_bias(dst, src, t, on_vector):
+            if on_vector:
+                nc.vector.tensor_scalar(dst, src, bf_col[:, t : t + 1], None, ADD)
+            else:
+                nc.scalar.activation(dst, src, IDENTITY, bias=bf_col[:, t : t + 1])
+
         def flux(n0, n, banks, vector_share):
             y = tile(f"y{n0}", [P, 4, n], F32)
+            sums = [bank[banks[t // 2]][:, (t % 2) * n : (t % 2 + 1) * n] for t in range(4)]
             for t in range(4):
-                nc.tensor.matmul_mx(
-                    out=bank[banks[t // 2]][:, (t % 2) * n : (t % 2 + 1) * n],
-                    lhsT=wf_q[:, 128 * t : 128 * (t + 1)].bitcast(FP8X4),
-                    lhsT_scale=wf_sc[:, 128 * t : 128 * (t + 1)],
-                    rhs=h_q[:, n0 : n0 + n].bitcast(FP8X4),
-                    rhs_scale=h_sc[:, n0 : n0 + n],
-                    start=True,
-                    stop=True,
-                )
+                flux_pass(sums[t], t, n0, n)
             for t in range(4):
-                src = bank[banks[t // 2]][:, (t % 2) * n : (t % 2 + 1) * n]
-                if t in vector_share:
-                    nc.vector.tensor_scalar(y[:, t, :], src, bf_col[:, t : t + 1], None, ADD)
-                else:
-                    nc.scalar.activation(y[:, t, :], src, IDENTITY, bias=bf_col[:, t : t + 1])
+                add_bias(y[:, t, :], sums[t], t, t in vector_share)
             nc.sync.dma_start(out=out_rows[:, :, n0 : n0 + n], in_=y[:])
+
+        def flux_first_half(t):
+            y = tile(f"y0_{t}", [P, HALF], F32)
+            sums = bank[(6, 7, 0, 1)[t]][:]
+            flux_pass(sums, t, 0, HALF)
+            add_bias(y[:], sums, t, False)
+            nc.sync.dma_start(out=out_rows[:, t, 0:HALF], in_=y[:])
+
+        def pair_bank(n0, jj):
+            return bank[2 * ((n0 - HALF) // 256) + jj]
 
         def a_pair(n0, jj):
             for j in (2 * jj, 2 * jj + 1):
                 for a in range(2):
-                    a_pass(bank[4 + jj][:, (j % 2) * 256 : (j % 2 + 1) * 256], a, j, n0, 256)
+                    a_pass(pair_bank(n0, jj)[:, (j % 2) * 256 : (j % 2 + 1) * 256], a, j, n0, 256)
 
         def multiply_pair(n0, jj):
             cols = slice(n0 - HALF, n0 - HALF + 256)
             nc.vector.tensor_tensor(
                 ab[1][:, 2 * jj : 2 * jj + 2, cols],
-                bank[4 + jj][:].rearrange("p (j n) -> p j n", j=2),
+                pair_bank(n0, jj)[:].rearrange("p (j n) -> p j n", j=2),
                 b_sb[1][:, 2 * jj : 2 * jj + 2, cols],
                 MULT,
             )
 
-        a_pair(512, 0)
-        a_pair(512, 1)
-        finish_h(0)
-        finish_h(1)
+        for n0 in (512, 768):
+            for jj in range(2):
+                a_pair(n0, jj)
+        for g in range(2):
+            finish_h(g)
+            c_group(g + 4)
+        quantize_h(0, 256)
         nc.vector.quantize_mx(out=wf_q[:].bitcast(FP8X4), scales=wf_sc[:], in_=wf_bf[:])
         finish_h(2)
-        quantize_h(0, 256)
-        flux(0, 256, (6, 7), ())
         finish_h(3)
         multiply_pair(512, 0)
-        a_pair(768, 0)
         quantize_h(256, 256)
-        flux(256, 256, (6, 7), ())
+        flux_first_half(0)
+        flux_first_half(1)
+        flux_first_half(2)
         multiply_pair(512, 1)
-        a_pair(768, 1)
+        flux_first_half(3)
+        c_group(6)
+        c_group(7)
         multiply_pair(768, 0)
         finish_h(4)
         finish_h(5)
         multiply_pair(768, 1)
         quantize_h(512, 256)
-        flux(512, 256, (6, 7), ())
+        flux(512, 256, (4, 5), ())
         finish_h(6)
         finish_h(7)
         quantize_h(768, 128)
-        flux(768, 128, (0, 1), ())
+        flux(768, 128, (0, 1), (2, 3))
         quantize_h(896, 128)
-        flux(896, 128, (4, 5), (2, 3))
+        flux(896, 128, (2, 3), (2, 3))

@@ -1,6 +1,7 @@
 from contextlib import ExitStack
 
 import concourse.mybir as mybir
+from concourse.masks import make_identity
 
 K, T, S, H, N = 1024, 4096, 1024, 512, 512
 FLOPS = 2 * S * (3 * K * H + H * N)
@@ -48,8 +49,9 @@ def tile_list_bilinear_flux_update_kernel(
         v_sc1 = tile("v_sc1", [P, S], U8)
         wb_raw = tile("wb_raw", [P, 2, 2 * H], U8)
         wc_raw = tile("wc_raw", [P, 2, H], I32)
-        bb_col = tile("bb_col", [P, 4], F32)
-        bf_col = tile("bf_col", [P, 4], F32)
+        bias_rows = tile("bias_rows", [P, P], F32)
+        identity = tile("identity", [P, P], F32)
+        bias = tile("bias", [P, 8], F32)
 
         nc.vector.memset(table_sc[:].bitcast(I32), 0)
         nc.vector.memset(wb_sc_raw[:].bitcast(I32), 0)
@@ -82,11 +84,14 @@ def tile_list_bilinear_flux_update_kernel(
         load_words(1, slice(2560, T))
         nc.sync.dma_start(out=wc_raw[:], in_=wc_words.rearrange("a p n i -> p a (n i)").bitcast(I32))
 
-        with nc.allow_non_contiguous_dma(reason="one bias value a partition"):
-            bb_rows = bb.rearrange("(u j e) -> e u j", j=4, e=4)
-            for e in range(4):
-                nc.gpsimd.dma_start(out=bb_col[e:P:4, :], in_=bb_rows[e])
-            nc.gpsimd.dma_start(out=bf_col[:], in_=bf.rearrange("(t p) -> p t", p=P))
+        nc.gpsimd.memset(bias_rows[:], 0.0)
+        nc.gpsimd.dma_start(
+            out=bias_rows[0:4, :].rearrange("j (u e) -> j u e", e=4), in_=bb.rearrange("(u j e) -> j u e", j=4, e=4)
+        )
+        nc.gpsimd.dma_start(out=bias_rows[4:8, :], in_=bf.rearrange("(t m) -> t m", t=4))
+        make_identity(nc, identity[:])
+        nc.tensor.transpose(bank[7][:, 0:P], bias_rows[:], identity[:])
+        nc.scalar.copy(bias[:], bank[7][:, 0:8])
 
         v = [
             [tile("v00", [P, HALF], U32), placed("v01", [P, HALF], U32, 41)],
@@ -144,12 +149,22 @@ def tile_list_bilinear_flux_update_kernel(
             for j in range(4):
                 b_pass(0, h, j)
 
-        b_sb = [tile(f"b_sb{h}", [P, 4, HALF], F32) for h in range(2)]
+        b_sb = [
+            [tile("b_sb00", [P, 2, HALF], F32), tile("b_sb01", [P, 2, HALF], F32)],
+            [tile("b_sb10", [P, 2, HALF], F32), placed("b_sb11", [P, 2, HALF], F32, 8)],
+        ]
+
+        def add_background(h, j):
+            nc.scalar.activation(
+                b_sb[h][j // 2][:, j % 2, :], bank[4 * h + j][:], IDENTITY, bias=bias[:, j : j + 1]
+            )
+
         for h in range(2):
             gather_words(1, h)
             for j in range(4):
                 b_pass(1, h, j)
-                nc.scalar.activation(b_sb[h][:, j, :], bank[4 * h + j][:], IDENTITY, bias=bb_col[:, j : j + 1])
+                if (h, j) < (1, 2):
+                    add_background(h, j)
 
         wf_raw = placed("wf_raw", [P, 4, N], F32, 29)
         wf_rows = wf.rearrange("(u j e) n -> e u j n", j=4, e=4)
@@ -176,7 +191,7 @@ def tile_list_bilinear_flux_update_kernel(
                         stop=(a == 1),
                     )
 
-        for g in range(4):
+        for g in range(2):
             c_group(g)
 
         wa_bf = [placed(f"wa_bf{a}", [P, 4 * H], BF16, 20 + 4 * a) for a in range(2)]
@@ -199,8 +214,13 @@ def tile_list_bilinear_flux_update_kernel(
         wa_src = [wa_raw[a][:].rearrange("p j (u t e) -> p t u j e", t=4, e=4) for a in range(2)]
         nc.vector.tensor_copy(wa_dst[0], wa_src[0])
         nc.vector.quantize_mx(out=wa_q[0][:].bitcast(FP8X4), scales=wa_sc[0][:], in_=wa_bf[0][:])
-        for j in range(4):
-            a_pass(bank[j][:], 0, j, 0, HALF)
+
+        def a_sums(c, j):
+            return bank[2 * (c % 2) + j // 2][:, (j % 2) * 256 : (j % 2 + 1) * 256]
+
+        for c in range(2):
+            for j in (0, 2):
+                a_pass(a_sums(c, j), 0, j, 256 * c, 256)
 
         for t in range(2):
             nc.vector.tensor_copy(wa_dst[1][:, t], wa_src[1][:, t])
@@ -212,13 +232,31 @@ def tile_list_bilinear_flux_update_kernel(
                 scales=wa_sc[1][:, 128 * j : 128 * (j + 1)],
                 in_=wa_bf[1][:, 512 * j : 512 * (j + 1)],
             )
-            a_pass(bank[j][:], 1, j, 0, HALF)
 
-        ab = [tile("ab0", [P, 4, HALF], F32), placed("ab1", [P, 4, HALF], F32, 29)]
-        for j, cols in ((0, slice(0, 512)), (1, slice(0, 512)), (2, slice(0, 512)), (3, slice(0, 256)), (3, slice(256, 512))):
-            nc.vector.tensor_tensor(ab[0][:, j, cols], bank[j][:, cols], b_sb[0][:, j, cols], MULT)
+        add_background(1, 2)
+        add_background(1, 3)
 
-        wf_bf = placed("wf_bf", [P, 4 * N], BF16, 43)
+        def a_pair(c, jj):
+            for j in (2 * jj, 2 * jj + 1):
+                for a in range(2):
+                    if not (c < 2 and j % 2 == 0 and a == 0):
+                        a_pass(a_sums(c, j), a, j, 256 * c, 256)
+
+        ab = [
+            tile(f"ab{c}", [P, 2, 256, 2], F32) if c < 2 else placed(f"ab{c}", [P, 2, 256, 2], F32, 21 + 4 * c)
+            for c in range(4)
+        ]
+
+        def multiply_pair(c, jj):
+            cols = slice(256 * (c % 2), 256 * (c % 2 + 1))
+            nc.vector.tensor_tensor(
+                ab[c][:, jj],
+                bank[2 * (c % 2) + jj][:].rearrange("p (e n) -> p n e", e=2),
+                b_sb[c // 2][jj][:, :, cols].rearrange("p e n -> p n e"),
+                MULT,
+            )
+
+        wf_bf = tile("wf_bf", [P, 4 * N], BF16)
         wf_q = tile("wf_q", [P, N], U32)
         wf_sc = tile("wf_sc", [P, N], U8)
         wf_dst = wf_bf[:].rearrange("p (c i j) -> p c j i", i=4, j=4)
@@ -226,19 +264,17 @@ def tile_list_bilinear_flux_update_kernel(
         for s in range(2):
             nc.scalar.copy(wf_dst[:, 64 * s : 64 * (s + 1)], wf_src[:, 64 * s : 64 * (s + 1)])
 
-        h_bf = [
-            placed("h_bf1", [P, 1024], BF16, 43) if c == 1 else tile(f"h_bf{c}", [P, 1024], BF16) for c in range(4)
-        ]
+        h_bf = tile("h_bf", [P, 4 * S], BF16)
         h_q = tile("h_q", [P, S], U32)
         h_sc = tile("h_sc", [P, S], U8)
         out_rows = out.rearrange("(t p) s -> p t s", p=P)
 
         def finish_h(g):
-            h, n0 = divmod(128 * g, HALF)
+            n0 = 128 * (g % 2)
             nc.vector.tensor_tensor(
-                h_bf[g // 2][:, 512 * (g % 2) : 512 * (g % 2 + 1)].rearrange("p (c i j) -> p c j i", i=2, j=4),
-                bank[4 + g % 4][:].rearrange("p (j c i) -> p c j i", j=4, i=2),
-                ab[h][:, :, n0 : n0 + 128].rearrange("p j (c i) -> p c j i", i=2),
+                h_bf[:, 512 * g : 512 * (g + 1)].rearrange("p (n jj e) -> p n jj e", jj=2, e=2),
+                bank[4 + g % 4][:].rearrange("p (jj e n) -> p n jj e", jj=2, e=2),
+                ab[g // 2][:, :, n0 : n0 + 128, :].rearrange("p jj n e -> p n jj e"),
                 ADD,
             )
 
@@ -246,7 +282,7 @@ def tile_list_bilinear_flux_update_kernel(
             nc.vector.quantize_mx(
                 out=h_q[:, n0 : n0 + n].bitcast(FP8X4),
                 scales=h_sc[:, n0 : n0 + n],
-                in_=h_bf[n0 // 256][:, 4 * (n0 % 256) : 4 * (n0 % 256 + n)],
+                in_=h_bf[:, 4 * n0 : 4 * (n0 + n)],
             )
 
         def flux_pass(dst, t, n0, n):
@@ -262,18 +298,20 @@ def tile_list_bilinear_flux_update_kernel(
 
         def add_bias(dst, src, t, on_vector):
             if on_vector:
-                nc.vector.tensor_scalar(dst, src, bf_col[:, t : t + 1], None, ADD)
+                nc.vector.tensor_scalar(dst, src, bias[:, 4 + t : 5 + t], None, ADD)
             else:
-                nc.scalar.activation(dst, src, IDENTITY, bias=bf_col[:, t : t + 1])
+                nc.scalar.activation(dst, src, IDENTITY, bias=bias[:, 4 + t : 5 + t])
 
-        def flux(n0, n, banks, vector_share):
+        def flux(n0, n, banks, vector_share, per_store):
             y = tile(f"y{n0}", [P, 4, n], F32)
             sums = [bank[banks[t // 2]][:, (t % 2) * n : (t % 2 + 1) * n] for t in range(4)]
             for t in range(4):
                 flux_pass(sums[t], t, n0, n)
             for t in range(4):
                 add_bias(y[:, t, :], sums[t], t, t in vector_share)
-            nc.sync.dma_start(out=out_rows[:, :, n0 : n0 + n], in_=y[:])
+                if (t + 1) % per_store == 0:
+                    rows = slice(t + 1 - per_store, t + 1)
+                    nc.sync.dma_start(out=out_rows[:, rows, n0 : n0 + n], in_=y[:, rows, :])
 
         def flux_first_half(t):
             y = tile(f"y0_{t}", [P, HALF], F32)
@@ -282,51 +320,45 @@ def tile_list_bilinear_flux_update_kernel(
             add_bias(y[:], sums, t, False)
             nc.sync.dma_start(out=out_rows[:, t, 0:HALF], in_=y[:])
 
-        def pair_bank(n0, jj):
-            return bank[2 * ((n0 - HALF) // 256) + jj]
-
-        def a_pair(n0, jj):
-            for j in (2 * jj, 2 * jj + 1):
-                for a in range(2):
-                    a_pass(pair_bank(n0, jj)[:, (j % 2) * 256 : (j % 2 + 1) * 256], a, j, n0, 256)
-
-        def multiply_pair(n0, jj):
-            cols = slice(n0 - HALF, n0 - HALF + 256)
-            nc.vector.tensor_tensor(
-                ab[1][:, 2 * jj : 2 * jj + 2, cols],
-                pair_bank(n0, jj)[:].rearrange("p (j n) -> p j n", j=2),
-                b_sb[1][:, 2 * jj : 2 * jj + 2, cols],
-                MULT,
-            )
-
-        for n0 in (512, 768):
+        for c in range(2):
             for jj in range(2):
-                a_pair(n0, jj)
-        for g in range(2):
-            finish_h(g)
-            c_group(g + 4)
-        quantize_h(0, 256)
-        nc.vector.quantize_mx(out=wf_q[:].bitcast(FP8X4), scales=wf_sc[:], in_=wf_bf[:])
+                a_pair(c, jj)
+        c_group(2)
+        c_group(3)
+        multiply_pair(0, 0)
+        multiply_pair(0, 1)
+        multiply_pair(1, 0)
+        finish_h(0)
+        multiply_pair(1, 1)
+        finish_h(1)
+        for jj in range(2):
+            a_pair(2, jj)
+        c_group(4)
+        c_group(5)
+        for jj in range(2):
+            a_pair(3, jj)
         finish_h(2)
+        quantize_h(0, 256)
         finish_h(3)
-        multiply_pair(512, 0)
         quantize_h(256, 256)
+        nc.vector.quantize_mx(out=wf_q[:].bitcast(FP8X4), scales=wf_sc[:], in_=wf_bf[:])
         flux_first_half(0)
         flux_first_half(1)
+        multiply_pair(2, 0)
         flux_first_half(2)
-        multiply_pair(512, 1)
+        multiply_pair(2, 1)
         flux_first_half(3)
         c_group(6)
         c_group(7)
-        multiply_pair(768, 0)
+        multiply_pair(3, 0)
         finish_h(4)
         finish_h(5)
-        multiply_pair(768, 1)
         quantize_h(512, 256)
-        flux(512, 256, (4, 5), ())
+        flux(512, 256, (4, 5), (), 2)
+        multiply_pair(3, 1)
         finish_h(6)
         finish_h(7)
         quantize_h(768, 128)
-        flux(768, 128, (0, 1), (2, 3))
+        flux(768, 128, (0, 1), (2, 3), 4)
         quantize_h(896, 128)
-        flux(896, 128, (2, 3), (2, 3))
+        flux(896, 128, (2, 3), (2, 3), 4)

@@ -41,97 +41,85 @@ def tile_list_bilinear_flux_update_kernel(
         bank = [psum.tile([P, 512], F32, name=f"bank{i}") for i in range(8)]
 
         offsets = lists.tile([P, S // 16], U16, name="offsets")
-        table = [placed(f"table{a}", [P, T], U32, 16 * a) for a in range(2)]
-        table_sc = placed("table_sc", [P, T], U8, 37)
-        wb_sc_raw = placed("wb_sc_raw", [P, 2, H], U8, 41)
+        table = [placed("table0", [P, T], U32, 0), tile("table1", [P, T], U32)]
+        table_sc = tile("table_sc", [P, T], U8)
+        picked_sc = tile("picked_sc", [P, S], U8)
+        v_sc = tile("v_sc", [P, 2 * S], U8)
+        wb_sc_raw = tile("wb_sc_raw", [P, 2, H], U8)
         wc_sc_raw = tile("wc_sc_raw", [P, 2, H], U8)
-        v_sc = tile("v_sc", [P, S], U8)
-        v_sc1 = tile("v_sc1", [P, S], U8)
         wb_raw = tile("wb_raw", [P, 2, 2 * H], U8)
         wc_raw = tile("wc_raw", [P, 2, H], I32)
+        wa_raw = [tile(f"wa_raw{a}", [P, 4, H], F32) for a in range(2)]
         bias_rows = tile("bias_rows", [P, P], F32)
         identity = tile("identity", [P, P], F32)
         bias = tile("bias", [P, 8], F32)
 
-        nc.vector.memset(table_sc[:].bitcast(I32), 0)
         nc.vector.memset(wb_sc_raw[:].bitcast(I32), 0)
+        nc.vector.memset(table_sc[32:64, :].bitcast(I32), 0)
+        nc.vector.memset(table_sc[64:P, :].bitcast(I32), 0)
         nc.vector.memset(wc_sc_raw[:].bitcast(I32), 0)
-        nc.vector.memset(v_sc1[:].bitcast(I32), 0)
+        nc.vector.memset(v_sc[:].bitcast(I32), 0)
 
-        def load_words(a, cols):
+        def load_words(a):
             words = tab_words[a].rearrange("p t i -> p (t i)").bitcast(I32)
-            nc.sync.dma_start(out=table[a][:, cols].bitcast(I32), in_=words[:, cols])
+            nc.sync.dma_start(out=table[a][:].bitcast(I32), in_=words)
 
-        def load_w_scales(engine, dst, src, row0):
+        def load_w_scales(dst, src, row0):
             for q in range(4):
-                engine.dma_start(
+                nc.gpsimd.dma_start(
                     out=dst[32 * q + row0 : 32 * q + row0 + 4, :, :].bitcast(I32),
                     in_=src[:, 4 * q : 4 * q + 4, :].rearrange("a r n -> r a n").bitcast(I32),
                 )
 
+        wa_rows = wa.rearrange("(a p j) c -> a p j c", a=2, j=4)
         nc.sync.dma_start(offsets[:], offs)
-        load_words(0, slice(0, 2048))
+        nc.sync.dma_start(out=table_sc[0:32, :].bitcast(I32), in_=tab_scales.rearrange("a q t -> q a t").bitcast(I32))
+        load_words(0)
         nc.sync.dma_start(out=wb_raw[:].bitcast(I32), in_=wb_words.rearrange("a p n -> p a n").bitcast(I32))
-        for q in range(4):
-            nc.sync.dma_start(
-                out=table_sc[32 * q : 32 * q + 8, :].bitcast(I32),
-                in_=tab_scales[:, 4 * q : 4 * q + 4, :].bitcast(I32),
-            )
-        load_words(0, slice(2048, T))
-        load_w_scales(nc.sync, wb_sc_raw, wb_scales, 0)
-        load_words(1, slice(0, 2560))
-        load_w_scales(nc.sync, wc_sc_raw, wc_scales, 4)
-        load_words(1, slice(2560, T))
+        load_words(1)
         nc.sync.dma_start(out=wc_raw[:], in_=wc_words.rearrange("a p n i -> p a (n i)").bitcast(I32))
+        for a in range(2):
+            nc.sync.dma_start(out=wa_raw[a][:], in_=wa_rows[a])
 
         nc.gpsimd.memset(bias_rows[:], 0.0)
+        load_w_scales(wb_sc_raw, wb_scales, 0)
         nc.gpsimd.dma_start(
-            out=bias_rows[0:4, :].rearrange("j (u e) -> j u e", e=4), in_=bb.rearrange("(u j e) -> j u e", j=4, e=4)
+            out=bias_rows[0:4, :].rearrange("t (g e) -> t g e", e=8), in_=bb.rearrange("(g t e) -> t g e", t=4, e=8)
         )
         nc.gpsimd.dma_start(out=bias_rows[4:8, :], in_=bf.rearrange("(t m) -> t m", t=4))
         make_identity(nc, identity[:])
+        load_w_scales(wc_sc_raw, wc_scales, 4)
         nc.tensor.transpose(bank[7][:, 0:P], bias_rows[:], identity[:])
         nc.scalar.copy(bias[:], bank[7][:, 0:8])
 
-        v = [
-            [tile("v00", [P, HALF], U32), placed("v01", [P, HALF], U32, 41)],
-            [tile("v10", [P, HALF], U32), tile("v11", [P, HALF], U32)],
-        ]
+        v = [[tile(f"v{a}{h}", [P, HALF], U32) for h in range(2)] for a in range(2)]
 
         def gather_words(a, h):
             nc.vector.tensor_copy(v[a][h][:], table[a][:].indirect(offsets[:, 32 * h : 32 * (h + 1)]))
 
         def v_plane(a, cols):
-            return v_sc[4 * a : P, cols]
+            return v_sc[:, S * a + cols.start : S * a + cols.stop]
 
-        nc.vector.tensor_copy(v_sc[:], table_sc[:].indirect(offsets[:]))
+        nc.vector.tensor_copy(picked_sc[:], table_sc[:].indirect(offsets[:]))
         for q in range(4):
-            nc.sync.dma_start(
-                out=v_sc1[32 * q : 32 * q + 4, :].bitcast(I32), in_=v_sc[32 * q + 4 : 32 * q + 8, :].bitcast(I32)
+            nc.scalar.dma_start(
+                out=v_sc[32 * q : 32 * q + 4, :].bitcast(I32), in_=picked_sc[8 * q : 8 * q + 8, :].bitcast(I32)
             )
 
         wb_q = tile("wb_q", [P, 2, 2 * H], U8)
-        wc_q = placed("wc_q", [P, 2, H], U32, 16)
-        w_sc = [tile("wb_sc", [P, 2, H], U8), placed("wc_sc", [P, 2, H], U8, 28)]
+        wc_q = tile("wc_q", [P, 2, H], U32)
+        w_sc = [tile("wb_sc", [P, 2, H], U8), tile("wc_sc", [P, 2, H], U8)]
 
-        def permute_scales(w):
+        def deal(dst, src, words):
             nc.vector.tensor_copy(
-                w_sc[w][:].bitcast(I32).rearrange("p a (t u) -> p a t u", t=4),
-                (wb_sc_raw, wc_sc_raw)[w][:].bitcast(I32).rearrange("p a (u t) -> p a t u", t=4),
+                dst.bitcast(I32).rearrange("p a (t g e) -> p a t g e", t=4, e=words),
+                src.bitcast(I32).rearrange("p a (g t e) -> p a t g e", t=4, e=words),
             )
 
+        deal(w_sc[0][:], wb_sc_raw[:], 2)
         gather_words(0, 0)
-        nc.vector.tensor_copy(
-            wb_q[:].bitcast(I32).rearrange("p a (t u e) -> p a t u e", t=4, e=2),
-            wb_raw[:].bitcast(I32).rearrange("p a (u t e) -> p a t u e", t=4, e=2),
-        )
-        permute_scales(0)
+        deal(wb_q[:], wb_raw[:], 4)
         gather_words(0, 1)
-
-        wa_raw = [placed(f"wa_raw{a}", [P, 4, H], F32, 8 * a) for a in range(2)]
-        wa_rows = wa.rearrange("(a p j) c -> a p j c", a=2, j=4)
-        for a in range(2):
-            nc.sync.dma_start(out=wa_raw[a][:], in_=wa_rows[a])
 
         def b_pass(a, h, j):
             cols = slice(h * HALF, (h + 1) * HALF)
@@ -140,7 +128,7 @@ def tile_list_bilinear_flux_update_kernel(
                 lhsT=wb_q[:, a, 256 * j : 256 * (j + 1)].bitcast(FP4X4),
                 lhsT_scale=w_sc[0][:, a, 128 * j : 128 * (j + 1)],
                 rhs=v[a][h][:].bitcast(FP8X4),
-                rhs_scale=(v_sc, v_sc1)[a][:, cols],
+                rhs_scale=v_plane(a, cols),
                 start=(a == 0),
                 stop=(a == 1),
             )
@@ -149,10 +137,7 @@ def tile_list_bilinear_flux_update_kernel(
             for j in range(4):
                 b_pass(0, h, j)
 
-        b_sb = [
-            [tile("b_sb00", [P, 2, HALF], F32), tile("b_sb01", [P, 2, HALF], F32)],
-            [tile("b_sb10", [P, 2, HALF], F32), placed("b_sb11", [P, 2, HALF], F32, 8)],
-        ]
+        b_sb = [[tile(f"b_sb{h}{jj}", [P, 2, HALF], F32) for jj in range(2)] for h in range(2)]
 
         def add_background(h, j):
             nc.scalar.activation(
@@ -163,26 +148,22 @@ def tile_list_bilinear_flux_update_kernel(
             gather_words(1, h)
             for j in range(4):
                 b_pass(1, h, j)
-                if (h, j) < (1, 2):
-                    add_background(h, j)
+                add_background(h, j)
 
-        wf_raw = placed("wf_raw", [P, 4, N], F32, 29)
-        wf_rows = wf.rearrange("(u j e) n -> e u j n", j=4, e=4)
-        for e in range(4):
-            nc.sync.dma_start(out=wf_raw[e:P:4, :, :], in_=wf_rows[e])
+        wf_raw = placed("wf_raw", [P, 4, N], F32, 0)
+        wf_rows = wf.rearrange("(g t e) n -> t g e n", t=4, e=8)
+        for t in range(4):
+            nc.sync.dma_start(out=wf_raw[:, t, :], in_=wf_rows[t])
 
-        nc.vector.tensor_copy(
-            wc_q[:].bitcast(I32).rearrange("p a (t u e) -> p a t u e", t=4, e=4),
-            wc_raw[:].rearrange("p a (u t e) -> p a t u e", t=4, e=4),
-        )
-        permute_scales(1)
+        deal(wc_q[:], wc_raw[:], 8)
+        deal(w_sc[1][:], wc_sc_raw[:], 2)
 
         def c_group(g):
             h, n0 = divmod(128 * g, HALF)
             for j in range(4):
                 for a in range(2):
                     nc.tensor.matmul_mx(
-                        out=bank[4 + g % 4][:, 128 * j : 128 * (j + 1)],
+                        out=bank[g % 4][:, 128 * j : 128 * (j + 1)],
                         lhsT=wc_q[:, a, 128 * j : 128 * (j + 1)].bitcast(FP8X4),
                         lhsT_scale=w_sc[1][4:P, a, 128 * j : 128 * (j + 1)],
                         rhs=v[a][h][:, n0 : n0 + 128].bitcast(FP8X4),
@@ -191,10 +172,10 @@ def tile_list_bilinear_flux_update_kernel(
                         stop=(a == 1),
                     )
 
-        for g in range(2):
+        for g in range(4):
             c_group(g)
 
-        wa_bf = [placed(f"wa_bf{a}", [P, 4 * H], BF16, 20 + 4 * a) for a in range(2)]
+        wa_bf = [tile(f"wa_bf{a}", [P, 4 * H], BF16) for a in range(2)]
         wa_q = [tile(f"wa_q{a}", [P, H], U32) for a in range(2)]
         wa_sc = [tile(f"wa_sc{a}", [P, H], U8) for a in range(2)]
 
@@ -210,13 +191,14 @@ def tile_list_bilinear_flux_update_kernel(
                 stop=(a == 1),
             )
 
-        wa_dst = [wa_bf[a][:].rearrange("p (t u e j) -> p t u j e", t=4, e=4, j=4) for a in range(2)]
-        wa_src = [wa_raw[a][:].rearrange("p j (u t e) -> p t u j e", t=4, e=4) for a in range(2)]
-        nc.vector.tensor_copy(wa_dst[0], wa_src[0])
+        wa_dst = [wa_bf[a][:].rearrange("p (t g f e j) -> p t g f j e", t=4, f=2, e=4, j=4) for a in range(2)]
+        wa_src = [wa_raw[a][:].rearrange("p j (g t f e) -> p t g f j e", t=4, f=2, e=4) for a in range(2)]
+        for t in range(4):
+            nc.vector.tensor_copy(wa_dst[0][:, t], wa_src[0][:, t])
         nc.vector.quantize_mx(out=wa_q[0][:].bitcast(FP8X4), scales=wa_sc[0][:], in_=wa_bf[0][:])
 
         def a_sums(c, j):
-            return bank[2 * (c % 2) + j // 2][:, (j % 2) * 256 : (j % 2 + 1) * 256]
+            return bank[4 + 2 * (c % 2) + j // 2][:, (j % 2) * 256 : (j % 2 + 1) * 256]
 
         for c in range(2):
             for j in (0, 2):
@@ -233,25 +215,19 @@ def tile_list_bilinear_flux_update_kernel(
                 in_=wa_bf[1][:, 512 * j : 512 * (j + 1)],
             )
 
-        add_background(1, 2)
-        add_background(1, 3)
-
         def a_pair(c, jj):
             for j in (2 * jj, 2 * jj + 1):
                 for a in range(2):
                     if not (c < 2 and j % 2 == 0 and a == 0):
                         a_pass(a_sums(c, j), a, j, 256 * c, 256)
 
-        ab = [
-            tile(f"ab{c}", [P, 2, 256, 2], F32) if c < 2 else placed(f"ab{c}", [P, 2, 256, 2], F32, 21 + 4 * c)
-            for c in range(4)
-        ]
+        ab = [tile(f"ab{c}", [P, 2, 256, 2], F32) for c in range(4)]
 
         def multiply_pair(c, jj):
             cols = slice(256 * (c % 2), 256 * (c % 2 + 1))
             nc.vector.tensor_tensor(
                 ab[c][:, jj],
-                bank[2 * (c % 2) + jj][:].rearrange("p (e n) -> p n e", e=2),
+                bank[4 + 2 * (c % 2) + jj][:].rearrange("p (e n) -> p n e", e=2),
                 b_sb[c // 2][jj][:, :, cols].rearrange("p e n -> p n e"),
                 MULT,
             )
@@ -273,7 +249,7 @@ def tile_list_bilinear_flux_update_kernel(
             n0 = 128 * (g % 2)
             nc.vector.tensor_tensor(
                 h_bf[:, 512 * g : 512 * (g + 1)].rearrange("p (n jj e) -> p n jj e", jj=2, e=2),
-                bank[4 + g % 4][:].rearrange("p (jj e n) -> p n jj e", jj=2, e=2),
+                bank[g % 4][:].rearrange("p (jj e n) -> p n jj e", jj=2, e=2),
                 ab[g // 2][:, :, n0 : n0 + 128, :].rearrange("p jj n e -> p n jj e"),
                 ADD,
             )
@@ -313,52 +289,41 @@ def tile_list_bilinear_flux_update_kernel(
                     rows = slice(t + 1 - per_store, t + 1)
                     nc.sync.dma_start(out=out_rows[:, rows, n0 : n0 + n], in_=y[:, rows, :])
 
-        def flux_first_half(t):
-            y = tile(f"y0_{t}", [P, HALF], F32)
-            sums = bank[(6, 7, 0, 1)[t]][:]
-            flux_pass(sums, t, 0, HALF)
-            add_bias(y[:], sums, t, False)
-            nc.sync.dma_start(out=out_rows[:, t, 0:HALF], in_=y[:])
-
         for c in range(2):
             for jj in range(2):
                 a_pair(c, jj)
-        c_group(2)
-        c_group(3)
         multiply_pair(0, 0)
         multiply_pair(0, 1)
         multiply_pair(1, 0)
         finish_h(0)
-        multiply_pair(1, 1)
         finish_h(1)
+        multiply_pair(1, 1)
         for jj in range(2):
             a_pair(2, jj)
         c_group(4)
         c_group(5)
         for jj in range(2):
             a_pair(3, jj)
-        finish_h(2)
         quantize_h(0, 256)
+        finish_h(2)
         finish_h(3)
-        quantize_h(256, 256)
         nc.vector.quantize_mx(out=wf_q[:].bitcast(FP8X4), scales=wf_sc[:], in_=wf_bf[:])
-        flux_first_half(0)
-        flux_first_half(1)
-        multiply_pair(2, 0)
-        flux_first_half(2)
-        multiply_pair(2, 1)
-        flux_first_half(3)
+        flux(0, 256, (2, 3), (), 4)
         c_group(6)
         c_group(7)
+        multiply_pair(2, 0)
+        quantize_h(256, 256)
+        multiply_pair(2, 1)
+        flux(256, 256, (4, 5), (), 4)
         multiply_pair(3, 0)
         finish_h(4)
         finish_h(5)
-        quantize_h(512, 256)
-        flux(512, 256, (4, 5), (), 2)
         multiply_pair(3, 1)
+        quantize_h(512, 256)
+        flux(512, 256, (0, 1), (), 2)
         finish_h(6)
         finish_h(7)
         quantize_h(768, 128)
-        flux(768, 128, (0, 1), (2, 3), 4)
+        flux(768, 128, (6, 7), (2, 3), 4)
         quantize_h(896, 128)
-        flux(896, 128, (2, 3), (2, 3), 4)
+        flux(896, 128, (4, 5), (2, 3), 4)

@@ -41,23 +41,23 @@ def tile_list_bilinear_flux_update_kernel(
         bank = [psum.tile([P, 512], F32, name=f"bank{i}") for i in range(8)]
 
         offsets = lists.tile([P, S // 16], U16, name="offsets")
-        table = [placed("table0", [P, T], U32, 0), tile("table1", [P, T], U32)]
-        table_sc = tile("table_sc", [P, T], U8)
+        table = [placed("table0", [P, T], U32, 0), placed("table1", [P, T], U32, 16)]
+        table_sc = placed("table_sc", [P, T], U8, 31)
         picked_sc = tile("picked_sc", [P, S], U8)
         v_sc = tile("v_sc", [P, 2 * S], U8)
         wb_sc_raw = tile("wb_sc_raw", [P, 2, H], U8)
-        wc_sc_raw = tile("wc_sc_raw", [P, 2, H], U8)
-        wb_raw = tile("wb_raw", [P, 2, 2 * H], U8)
-        wc_raw = tile("wc_raw", [P, 2, H], I32)
-        wa_raw = [tile(f"wa_raw{a}", [P, 4, H], F32) for a in range(2)]
+        wc_sc_raw = placed("wc_sc_raw", [P, 2, H], U8, 32)
+        wb_raw = placed("wb_raw", [P, 2, 2 * H], U8, 44)
+        wc_raw = placed("wc_raw", [P, 2, H], I32, 33)
+        wa_raw = [placed(f"wa_raw{a}", [P, 4, H], F32, 37 + 8 * a) for a in range(2)]
         bias_rows = tile("bias_rows", [P, P], F32)
         identity = tile("identity", [P, P], F32)
         bias = tile("bias", [P, 8], F32)
 
-        nc.vector.memset(wb_sc_raw[:].bitcast(I32), 0)
         nc.vector.memset(table_sc[32:64, :].bitcast(I32), 0)
         nc.vector.memset(table_sc[64:P, :].bitcast(I32), 0)
-        nc.vector.memset(wc_sc_raw[:].bitcast(I32), 0)
+        w_sc = [tile("wb_sc", [P, 2, H], U8), tile("wc_sc", [P, 2, H], U8)]
+        nc.vector.memset(w_sc[0][:].bitcast(I32), 0)
         nc.vector.memset(v_sc[:].bitcast(I32), 0)
 
         def load_words(a):
@@ -66,7 +66,7 @@ def tile_list_bilinear_flux_update_kernel(
 
         def load_w_scales(dst, src, row0):
             for q in range(4):
-                nc.gpsimd.dma_start(
+                nc.sync.dma_start(
                     out=dst[32 * q + row0 : 32 * q + row0 + 4, :, :].bitcast(I32),
                     in_=src[:, 4 * q : 4 * q + 4, :].rearrange("a r n -> r a n").bitcast(I32),
                 )
@@ -74,21 +74,16 @@ def tile_list_bilinear_flux_update_kernel(
         wa_rows = wa.rearrange("(a p j) c -> a p j c", a=2, j=4)
         nc.sync.dma_start(offsets[:], offs)
         nc.sync.dma_start(out=table_sc[0:32, :].bitcast(I32), in_=tab_scales.rearrange("a q t -> q a t").bitcast(I32))
-        load_words(0)
         nc.sync.dma_start(out=wb_raw[:].bitcast(I32), in_=wb_words.rearrange("a p n -> p a n").bitcast(I32))
-        load_words(1)
-        nc.sync.dma_start(out=wc_raw[:], in_=wc_words.rearrange("a p n i -> p a (n i)").bitcast(I32))
-        for a in range(2):
-            nc.sync.dma_start(out=wa_raw[a][:], in_=wa_rows[a])
+        load_w_scales(wb_sc_raw, wb_scales, 0)
+        load_words(0)
 
         nc.gpsimd.memset(bias_rows[:], 0.0)
-        load_w_scales(wb_sc_raw, wb_scales, 0)
         nc.gpsimd.dma_start(
             out=bias_rows[0:4, :].rearrange("t (g e) -> t g e", e=8), in_=bb.rearrange("(g t e) -> t g e", t=4, e=8)
         )
         nc.gpsimd.dma_start(out=bias_rows[4:8, :], in_=bf.rearrange("(t m) -> t m", t=4))
         make_identity(nc, identity[:])
-        load_w_scales(wc_sc_raw, wc_scales, 4)
         nc.tensor.transpose(bank[7][:, 0:P], bias_rows[:], identity[:])
         nc.scalar.copy(bias[:], bank[7][:, 0:8])
 
@@ -102,13 +97,16 @@ def tile_list_bilinear_flux_update_kernel(
 
         nc.vector.tensor_copy(picked_sc[:], table_sc[:].indirect(offsets[:]))
         for q in range(4):
-            nc.scalar.dma_start(
+            nc.sync.dma_start(
                 out=v_sc[32 * q : 32 * q + 4, :].bitcast(I32), in_=picked_sc[8 * q : 8 * q + 8, :].bitcast(I32)
             )
+        nc.vector.memset(wc_sc_raw[:].bitcast(I32), 0)
+        load_words(1)
+        nc.sync.dma_start(out=wc_raw[:], in_=wc_words.rearrange("a p n i -> p a (n i)").bitcast(I32))
+        load_w_scales(wc_sc_raw, wc_scales, 4)
 
         wb_q = tile("wb_q", [P, 2, 2 * H], U8)
         wc_q = tile("wc_q", [P, 2, H], U32)
-        w_sc = [tile("wb_sc", [P, 2, H], U8), tile("wc_sc", [P, 2, H], U8)]
 
         def deal(dst, src, words):
             nc.vector.tensor_copy(
@@ -116,9 +114,12 @@ def tile_list_bilinear_flux_update_kernel(
                 src.bitcast(I32).rearrange("p a (g t e) -> p a t g e", t=4, e=words),
             )
 
-        deal(w_sc[0][:], wb_sc_raw[:], 2)
-        gather_words(0, 0)
+        for q in range(4):
+            deal(w_sc[0][32 * q : 32 * q + 4], wb_sc_raw[32 * q : 32 * q + 4], 2)
         deal(wb_q[:], wb_raw[:], 4)
+        for a in range(2):
+            nc.sync.dma_start(out=wa_raw[a][:], in_=wa_rows[a])
+        gather_words(0, 0)
         gather_words(0, 1)
 
         def b_pass(a, h, j):

@@ -159,12 +159,15 @@ def tile_list_bilinear_flux_update_kernel(
         deal(wc_q[:], wc_raw[:], 8)
         deal(w_sc[1][:], wc_sc_raw[:], 2)
 
+        c_bank = (0, 1, 2, 3, 0, 1, 6, 7)
+        a_bank = (4, 6, 4, 2)
+
         def c_group(g):
             h, n0 = divmod(128 * g, HALF)
             for j in range(4):
                 for a in range(2):
                     nc.tensor.matmul_mx(
-                        out=bank[g % 4][:, 128 * j : 128 * (j + 1)],
+                        out=bank[c_bank[g]][:, 128 * j : 128 * (j + 1)],
                         lhsT=wc_q[:, a, 128 * j : 128 * (j + 1)].bitcast(FP8X4),
                         lhsT_scale=w_sc[1][4:P, a, 128 * j : 128 * (j + 1)],
                         rhs=v[a][h][:, n0 : n0 + 128].bitcast(FP8X4),
@@ -180,16 +183,17 @@ def tile_list_bilinear_flux_update_kernel(
         wa_q = [tile(f"wa_q{a}", [P, H], U32) for a in range(2)]
         wa_sc = [tile(f"wa_sc{a}", [P, H], U8) for a in range(2)]
 
-        def a_pass(dst, a, j, n0, n):
+        def a_pass(c, a, j):
+            n0, n = 256 * c, 256
             h, m0 = divmod(n0, HALF)
             nc.tensor.matmul_mx(
-                out=dst,
+                out=bank[a_bank[c] + j // 2][:, (j % 2) * 256 : (j % 2 + 1) * 256],
                 lhsT=wa_q[a][:, 128 * j : 128 * (j + 1)].bitcast(FP8X4),
                 lhsT_scale=wa_sc[a][:, 128 * j : 128 * (j + 1)],
                 rhs=v[a][h][:, m0 : m0 + n].bitcast(FP8X4),
                 rhs_scale=v_plane(a, slice(n0, n0 + n)),
-                start=(a == 0),
-                stop=(a == 1),
+                start=(a == 0 and j % 2 == 0),
+                stop=(a == 1 and j % 2 == 1),
             )
 
         wa_dst = [wa_bf[a][:].rearrange("p (t g f e j) -> p t g f j e", t=4, f=2, e=4, j=4) for a in range(2)]
@@ -198,17 +202,13 @@ def tile_list_bilinear_flux_update_kernel(
             nc.vector.tensor_copy(wa_dst[0][:, t], wa_src[0][:, t])
         nc.vector.quantize_mx(out=wa_q[0][:].bitcast(FP8X4), scales=wa_sc[0][:], in_=wa_bf[0][:])
 
-        def a_sums(c, j):
-            return bank[4 + 2 * (c % 2) + j // 2][:, (j % 2) * 256 : (j % 2 + 1) * 256]
-
         for c in range(2):
-            for j in (0, 2):
-                a_pass(a_sums(c, j), 0, j, 256 * c, 256)
+            for j in range(4):
+                a_pass(c, 0, j)
 
-        for t in range(2):
+        for t in range(3):
             nc.vector.tensor_copy(wa_dst[1][:, t], wa_src[1][:, t])
-        for t in range(2, 4):
-            nc.scalar.copy(wa_dst[1][:, t], wa_src[1][:, t])
+        nc.scalar.copy(wa_dst[1][:, 3], wa_src[1][:, 3])
         for j in range(4):
             nc.vector.quantize_mx(
                 out=wa_q[1][:, 128 * j : 128 * (j + 1)].bitcast(FP8X4),
@@ -217,10 +217,9 @@ def tile_list_bilinear_flux_update_kernel(
             )
 
         def a_pair(c, jj):
-            for j in (2 * jj, 2 * jj + 1):
-                for a in range(2):
-                    if not (c < 2 and j % 2 == 0 and a == 0):
-                        a_pass(a_sums(c, j), a, j, 256 * c, 256)
+            for a in range(1 if c < 2 else 0, 2):
+                for j in (2 * jj, 2 * jj + 1):
+                    a_pass(c, a, j)
 
         ab = [tile(f"ab{c}", [P, 2, 256, 2], F32) for c in range(4)]
 
@@ -228,7 +227,7 @@ def tile_list_bilinear_flux_update_kernel(
             cols = slice(256 * (c % 2), 256 * (c % 2 + 1))
             nc.vector.tensor_tensor(
                 ab[c][:, jj],
-                bank[4 + 2 * (c % 2) + jj][:].rearrange("p (e n) -> p n e", e=2),
+                bank[a_bank[c] + jj][:].rearrange("p (e n) -> p n e", e=2),
                 b_sb[c // 2][jj][:, :, cols].rearrange("p e n -> p n e"),
                 MULT,
             )
@@ -250,7 +249,7 @@ def tile_list_bilinear_flux_update_kernel(
             n0 = 128 * (g % 2)
             nc.vector.tensor_tensor(
                 h_bf[:, 512 * g : 512 * (g + 1)].rearrange("p (n jj e) -> p n jj e", jj=2, e=2),
-                bank[g % 4][:].rearrange("p (jj e n) -> p n jj e", jj=2, e=2),
+                bank[c_bank[g]][:].rearrange("p (jj e n) -> p n jj e", jj=2, e=2),
                 ab[g // 2][:, :, n0 : n0 + 128, :].rearrange("p jj n e -> p n jj e"),
                 ADD,
             )
@@ -303,19 +302,19 @@ def tile_list_bilinear_flux_update_kernel(
             a_pair(2, jj)
         c_group(4)
         c_group(5)
-        for jj in range(2):
-            a_pair(3, jj)
         quantize_h(0, 256)
+        nc.vector.quantize_mx(out=wf_q[:].bitcast(FP8X4), scales=wf_sc[:], in_=wf_bf[:])
+        flux(0, 256, (6, 7), (), 2)
         finish_h(2)
         finish_h(3)
-        nc.vector.quantize_mx(out=wf_q[:].bitcast(FP8X4), scales=wf_sc[:], in_=wf_bf[:])
-        flux(0, 256, (2, 3), (), 4)
+        for jj in range(2):
+            a_pair(3, jj)
         c_group(6)
         c_group(7)
         multiply_pair(2, 0)
         quantize_h(256, 256)
         multiply_pair(2, 1)
-        flux(256, 256, (4, 5), (), 4)
+        flux(256, 256, (4, 5), (), 2)
         multiply_pair(3, 0)
         finish_h(4)
         finish_h(5)
@@ -325,6 +324,6 @@ def tile_list_bilinear_flux_update_kernel(
         finish_h(6)
         finish_h(7)
         quantize_h(768, 128)
-        flux(768, 128, (6, 7), (2, 3), 4)
+        flux(768, 128, (2, 3), (2, 3), 4)
         quantize_h(896, 128)
         flux(896, 128, (4, 5), (2, 3), 4)

@@ -159,8 +159,8 @@ def tile_list_bilinear_flux_update_kernel(
         deal(wc_q[:], wc_raw[:], 8)
         deal(w_sc[1][:], wc_sc_raw[:], 2)
 
-        c_bank = (0, 1, 2, 3, 0, 1, 6, 7)
-        a_bank = (4, 6, 4, 2)
+        c_bank = (0, 1, 2, 3, 4, 5, 6, 7)
+        a_bank = (4, 6, 0, 2)
 
         def c_group(g):
             h, n0 = divmod(128 * g, HALF)
@@ -176,7 +176,22 @@ def tile_list_bilinear_flux_update_kernel(
                         stop=(a == 1),
                     )
 
-        for g in range(4):
+        c_sb = tile("c_sb", [P, 2, 256, 2], F32)
+        for jj in range(2):
+            for e in range(2):
+                j = 2 * jj + e
+                for a in range(2):
+                    nc.tensor.matmul_mx(
+                        out=bank[jj][:, 256 * e : 256 * (e + 1)],
+                        lhsT=wc_q[:, a, 128 * j : 128 * (j + 1)].bitcast(FP8X4),
+                        lhsT_scale=w_sc[1][4:P, a, 128 * j : 128 * (j + 1)],
+                        rhs=v[a][0][:, 0:256].bitcast(FP8X4),
+                        rhs_scale=v_plane(a, slice(0, 256)),
+                        start=(a == 0),
+                        stop=(a == 1),
+                    )
+            nc.scalar.copy(c_sb[:, jj], bank[jj][:].rearrange("p (e n) -> p n e", e=2))
+        for g in range(2, 4):
             c_group(g)
 
         wa_bf = [tile(f"wa_bf{a}", [P, 4 * H], BF16) for a in range(2)]
@@ -192,8 +207,8 @@ def tile_list_bilinear_flux_update_kernel(
                 lhsT_scale=wa_sc[a][:, 128 * j : 128 * (j + 1)],
                 rhs=v[a][h][:, m0 : m0 + n].bitcast(FP8X4),
                 rhs_scale=v_plane(a, slice(n0, n0 + n)),
-                start=(a == 0 and j % 2 == 0),
-                stop=(a == 1 and j % 2 == 1),
+                start=(a == (0 if c < 2 else 1) and j % 2 == 0),
+                stop=(a == (1 if c < 2 else 0) and j % 2 == 1),
             )
 
         wa_dst = [wa_bf[a][:].rearrange("p (t g f e j) -> p t g f j e", t=4, f=2, e=4, j=4) for a in range(2)]
@@ -206,18 +221,18 @@ def tile_list_bilinear_flux_update_kernel(
             for j in range(4):
                 a_pass(c, 0, j)
 
-        for t in range(3):
-            nc.vector.tensor_copy(wa_dst[1][:, t], wa_src[1][:, t])
-        nc.scalar.copy(wa_dst[1][:, 3], wa_src[1][:, 3])
-        for j in range(4):
-            nc.vector.quantize_mx(
-                out=wa_q[1][:, 128 * j : 128 * (j + 1)].bitcast(FP8X4),
-                scales=wa_sc[1][:, 128 * j : 128 * (j + 1)],
-                in_=wa_bf[1][:, 512 * j : 512 * (j + 1)],
-            )
+        for jj in range(2):
+            for j in (2 * jj, 2 * jj + 1):
+                nc.vector.tensor_copy(wa_dst[1][:, j], wa_src[1][:, j])
+            for j in (2 * jj, 2 * jj + 1):
+                nc.vector.quantize_mx(
+                    out=wa_q[1][:, 128 * j : 128 * (j + 1)].bitcast(FP8X4),
+                    scales=wa_sc[1][:, 128 * j : 128 * (j + 1)],
+                    in_=wa_bf[1][:, 512 * j : 512 * (j + 1)],
+                )
 
         def a_pair(c, jj):
-            for a in range(1 if c < 2 else 0, 2):
+            for a in (1,) if c < 2 else (1, 0):
                 for j in (2 * jj, 2 * jj + 1):
                     a_pass(c, a, j)
 
@@ -252,6 +267,11 @@ def tile_list_bilinear_flux_update_kernel(
                 bank[c_bank[g]][:].rearrange("p (jj e n) -> p n jj e", jj=2, e=2),
                 ab[g // 2][:, :, n0 : n0 + 128, :].rearrange("p jj n e -> p n jj e"),
                 ADD,
+            )
+
+        def finish_first_chunk(jj):
+            nc.gpsimd.tensor_tensor(
+                h_bf[:, 0:1024].rearrange("p (n jj e) -> p jj n e", jj=2, e=2)[:, jj], ab[0][:, jj], c_sb[:, jj], ADD
             )
 
         def quantize_h(n0, n):
@@ -289,41 +309,38 @@ def tile_list_bilinear_flux_update_kernel(
                     rows = slice(t + 1 - per_store, t + 1)
                     nc.sync.dma_start(out=out_rows[:, rows, n0 : n0 + n], in_=y[:, rows, :])
 
-        for c in range(2):
+        for c in range(3):
             for jj in range(2):
                 a_pair(c, jj)
-        multiply_pair(0, 0)
-        multiply_pair(0, 1)
-        multiply_pair(1, 0)
-        finish_h(0)
-        finish_h(1)
-        multiply_pair(1, 1)
         for jj in range(2):
-            a_pair(2, jj)
+            multiply_pair(0, jj)
+            finish_first_chunk(jj)
         c_group(4)
         c_group(5)
+        multiply_pair(1, 0)
+        multiply_pair(1, 1)
+        multiply_pair(2, 0)
+        finish_h(2)
         quantize_h(0, 256)
         nc.vector.quantize_mx(out=wf_q[:].bitcast(FP8X4), scales=wf_sc[:], in_=wf_bf[:])
         flux(0, 256, (6, 7), (), 2)
-        finish_h(2)
         finish_h(3)
         for jj in range(2):
             a_pair(3, jj)
         c_group(6)
         c_group(7)
-        multiply_pair(2, 0)
-        quantize_h(256, 256)
         multiply_pair(2, 1)
-        flux(256, 256, (4, 5), (), 2)
+        quantize_h(256, 256)
+        flux(256, 256, (0, 1), (), 2)
         multiply_pair(3, 0)
         finish_h(4)
         finish_h(5)
         multiply_pair(3, 1)
         quantize_h(512, 256)
-        flux(512, 256, (0, 1), (), 2)
+        flux(512, 256, (2, 3), (), 2)
         finish_h(6)
         finish_h(7)
         quantize_h(768, 128)
-        flux(768, 128, (2, 3), (2, 3), 4)
+        flux(768, 128, (4, 5), (2, 3), 4)
         quantize_h(896, 128)
-        flux(896, 128, (4, 5), (2, 3), 4)
+        flux(896, 128, (0, 1), (2, 3), 4)

@@ -159,8 +159,8 @@ def tile_list_bilinear_flux_update_kernel(
         deal(wc_q[:], wc_raw[:], 8)
         deal(w_sc[1][:], wc_sc_raw[:], 2)
 
-        c_bank = (0, 1, 2, 3, 4, 5, 6, 7)
-        a_bank = (4, 6, 0, 2)
+        c_bank = (0, 1, 2, 3, 4, 5, 3, 0)
+        a_bank = ((4, 5), (6, 7), (2, 3), (4, 2))
 
         def c_group(g):
             h, n0 = divmod(128 * g, HALF)
@@ -202,13 +202,13 @@ def tile_list_bilinear_flux_update_kernel(
             n0, n = 256 * c, 256
             h, m0 = divmod(n0, HALF)
             nc.tensor.matmul_mx(
-                out=bank[a_bank[c] + j // 2][:, (j % 2) * 256 : (j % 2 + 1) * 256],
+                out=bank[a_bank[c][j // 2]][:, (j % 2) * 256 : (j % 2 + 1) * 256],
                 lhsT=wa_q[a][:, 128 * j : 128 * (j + 1)].bitcast(FP8X4),
                 lhsT_scale=wa_sc[a][:, 128 * j : 128 * (j + 1)],
                 rhs=v[a][h][:, m0 : m0 + n].bitcast(FP8X4),
                 rhs_scale=v_plane(a, slice(n0, n0 + n)),
-                start=(a == (0 if c < 2 else 1) and j % 2 == 0),
-                stop=(a == (1 if c < 2 else 0) and j % 2 == 1),
+                start=(a == (0 if c == 0 else 1) and j % 2 == 0),
+                stop=(a == (1 if c == 0 else 0) and j % 2 == 1),
             )
 
         wa_dst = [wa_bf[a][:].rearrange("p (t g f e j) -> p t g f j e", t=4, f=2, e=4, j=4) for a in range(2)]
@@ -217,32 +217,31 @@ def tile_list_bilinear_flux_update_kernel(
             nc.vector.tensor_copy(wa_dst[0][:, t], wa_src[0][:, t])
         nc.vector.quantize_mx(out=wa_q[0][:].bitcast(FP8X4), scales=wa_sc[0][:], in_=wa_bf[0][:])
 
-        for c in range(2):
-            for j in range(4):
-                a_pass(c, 0, j)
+        for j in range(4):
+            a_pass(0, 0, j)
 
-        for jj in range(2):
-            for j in (2 * jj, 2 * jj + 1):
-                nc.vector.tensor_copy(wa_dst[1][:, j], wa_src[1][:, j])
-            for j in (2 * jj, 2 * jj + 1):
+        for js in ((0, 1, 2), (3,)):
+            for j in js:
+                nc.vector.tensor_copy(wa_dst[1][:, j % 3], wa_src[1][:, j])
+            for j in (0, 1) if 0 in js else (2, 3):
                 nc.vector.quantize_mx(
                     out=wa_q[1][:, 128 * j : 128 * (j + 1)].bitcast(FP8X4),
                     scales=wa_sc[1][:, 128 * j : 128 * (j + 1)],
-                    in_=wa_bf[1][:, 512 * j : 512 * (j + 1)],
+                    in_=wa_bf[1][:, 512 * (j % 3) : 512 * (j % 3 + 1)],
                 )
 
         def a_pair(c, jj):
-            for a in (1,) if c < 2 else (1, 0):
+            for a in (1,) if c == 0 else (1, 0):
                 for j in (2 * jj, 2 * jj + 1):
                     a_pass(c, a, j)
 
         ab = [tile(f"ab{c}", [P, 2, 256, 2], F32) for c in range(4)]
 
-        def multiply_pair(c, jj):
-            cols = slice(256 * (c % 2), 256 * (c % 2 + 1))
+        def multiply_pair(c, jj, n0=0, n=256):
+            cols = slice(256 * (c % 2) + n0, 256 * (c % 2) + n0 + n)
             nc.vector.tensor_tensor(
-                ab[c][:, jj],
-                bank[a_bank[c] + jj][:].rearrange("p (e n) -> p n e", e=2),
+                ab[c][:, jj, n0 : n0 + n],
+                bank[a_bank[c][jj]][:].rearrange("p (e n) -> p n e", e=2)[:, n0 : n0 + n],
                 b_sb[c // 2][jj][:, :, cols].rearrange("p e n -> p n e"),
                 MULT,
             )
@@ -274,6 +273,16 @@ def tile_list_bilinear_flux_update_kernel(
                 h_bf[:, 0:1024].rearrange("p (n jj e) -> p jj n e", jj=2, e=2)[:, jj], ab[0][:, jj], c_sb[:, jj], ADD
             )
 
+        c4_sb = tile("c4_sb", [P, 2, 128, 2], F32)
+
+        def finish_fifth_group(jj):
+            nc.gpsimd.tensor_tensor(
+                h_bf[:, 2048:2560].rearrange("p (n jj e) -> p jj n e", jj=2, e=2)[:, jj],
+                ab[2][:, jj, 0:128],
+                c4_sb[:, jj],
+                ADD,
+            )
+
         def quantize_h(n0, n):
             nc.vector.quantize_mx(
                 out=h_q[:, n0 : n0 + n].bitcast(FP8X4),
@@ -300,7 +309,8 @@ def tile_list_bilinear_flux_update_kernel(
 
         def flux(n0, n, banks, vector_share, per_store):
             y = tile(f"y{n0}", [P, 4, n], F32)
-            sums = [bank[banks[t // 2]][:, (t % 2) * n : (t % 2 + 1) * n] for t in range(4)]
+            per_bank = 4 // len(banks)
+            sums = [bank[banks[t // per_bank]][:, (t % per_bank) * n : (t % per_bank + 1) * n] for t in range(4)]
             for t in range(4):
                 flux_pass(sums[t], t, n0, n)
             for t in range(4):
@@ -309,38 +319,40 @@ def tile_list_bilinear_flux_update_kernel(
                     rows = slice(t + 1 - per_store, t + 1)
                     nc.sync.dma_start(out=out_rows[:, rows, n0 : n0 + n], in_=y[:, rows, :])
 
-        for c in range(3):
+        for c in range(2):
             for jj in range(2):
                 a_pair(c, jj)
         for jj in range(2):
             multiply_pair(0, jj)
             finish_first_chunk(jj)
         c_group(4)
+        nc.scalar.copy(c4_sb[:], bank[c_bank[4]][:].rearrange("p (jj e n) -> p jj n e", jj=2, e=2))
         c_group(5)
         multiply_pair(1, 0)
-        multiply_pair(1, 1)
-        multiply_pair(2, 0)
+        multiply_pair(1, 1, 0, 128)
+        multiply_pair(1, 1, 128, 128)
         finish_h(2)
-        quantize_h(0, 256)
-        nc.vector.quantize_mx(out=wf_q[:].bitcast(FP8X4), scales=wf_sc[:], in_=wf_bf[:])
-        flux(0, 256, (6, 7), (), 2)
         finish_h(3)
+        for jj in range(2):
+            a_pair(2, jj)
+        nc.vector.quantize_mx(out=wf_q[:].bitcast(FP8X4), scales=wf_sc[:], in_=wf_bf[:])
+        quantize_h(0, 512)
+        flux(0, 512, (0, 1, 6, 7), (), 1)
+        for jj in range(2):
+            multiply_pair(2, jj)
+            finish_fifth_group(jj)
         for jj in range(2):
             a_pair(3, jj)
         c_group(6)
         c_group(7)
-        multiply_pair(2, 1)
-        quantize_h(256, 256)
-        flux(256, 256, (0, 1), (), 2)
         multiply_pair(3, 0)
-        finish_h(4)
         finish_h(5)
         multiply_pair(3, 1)
         quantize_h(512, 256)
-        flux(512, 256, (2, 3), (), 2)
+        flux(512, 256, (4, 5), (), 2)
         finish_h(6)
         finish_h(7)
         quantize_h(768, 128)
-        flux(768, 128, (4, 5), (2, 3), 4)
+        flux(768, 128, (1, 6), (2, 3), 4)
         quantize_h(896, 128)
-        flux(896, 128, (0, 1), (2, 3), 4)
+        flux(896, 128, (7, 2), (2, 3), 4)

@@ -20,6 +20,7 @@ IDENTITY = mybir.ActivationFunctionType.Identity
 
 P = 128
 HALF = 512
+AHEAD = 1024
 
 
 def tile_list_bilinear_flux_update_kernel(
@@ -60,9 +61,9 @@ def tile_list_bilinear_flux_update_kernel(
         nc.vector.memset(w_sc[0][:].bitcast(I32), 0)
         nc.vector.memset(v_sc[:].bitcast(I32), 0)
 
-        def load_words(a):
+        def load_words(a, t0, t1):
             words = tab_words[a].rearrange("p t i -> p (t i)").bitcast(I32)
-            nc.sync.dma_start(out=table[a][:].bitcast(I32), in_=words)
+            nc.sync.dma_start(out=table[a][:, t0:t1].bitcast(I32), in_=words[:, t0:t1])
 
         def load_w_scales(dst, src, row0):
             for q in range(4):
@@ -76,7 +77,8 @@ def tile_list_bilinear_flux_update_kernel(
         nc.sync.dma_start(out=table_sc[0:32, :].bitcast(I32), in_=tab_scales.rearrange("a q t -> q a t").bitcast(I32))
         nc.sync.dma_start(out=wb_raw[:].bitcast(I32), in_=wb_words.rearrange("a p n -> p a n").bitcast(I32))
         load_w_scales(wb_sc_raw, wb_scales, 0)
-        load_words(0)
+        load_words(0, 0, T)
+        load_words(1, 0, AHEAD)
 
         nc.gpsimd.memset(bias_rows[:], 0.0)
         nc.gpsimd.dma_start(
@@ -96,12 +98,12 @@ def tile_list_bilinear_flux_update_kernel(
             return v_sc[:, S * a + cols.start : S * a + cols.stop]
 
         nc.vector.tensor_copy(picked_sc[:], table_sc[:].indirect(offsets[:]))
-        for q in range(4):
+        for q in (0, 2, 1, 3):
             nc.sync.dma_start(
                 out=v_sc[32 * q : 32 * q + 4, :].bitcast(I32), in_=picked_sc[8 * q : 8 * q + 8, :].bitcast(I32)
             )
         nc.vector.memset(wc_sc_raw[:].bitcast(I32), 0)
-        load_words(1)
+        load_words(1, AHEAD, T)
         nc.sync.dma_start(out=wc_raw[:], in_=wc_words.rearrange("a p n i -> p a (n i)").bitcast(I32))
         load_w_scales(wc_sc_raw, wc_scales, 4)
 
@@ -307,7 +309,7 @@ def tile_list_bilinear_flux_update_kernel(
             else:
                 nc.scalar.activation(dst, src, IDENTITY, bias=bias[:, 4 + t : 5 + t])
 
-        def flux(n0, n, banks, vector_share, per_store):
+        def flux(n0, n, banks, vector_share, stores):
             y = tile(f"y{n0}", [P, 4, n], F32)
             per_bank = 4 // len(banks)
             sums = [bank[banks[t // per_bank]][:, (t % per_bank) * n : (t % per_bank + 1) * n] for t in range(4)]
@@ -315,8 +317,8 @@ def tile_list_bilinear_flux_update_kernel(
                 flux_pass(sums[t], t, n0, n)
             for t in range(4):
                 add_bias(y[:, t, :], sums[t], t, t in vector_share)
-                if (t + 1) % per_store == 0:
-                    rows = slice(t + 1 - per_store, t + 1)
+                if t + 1 in stores:
+                    rows = slice(max([0] + [end for end in stores if end <= t]), t + 1)
                     nc.sync.dma_start(out=out_rows[:, rows, n0 : n0 + n], in_=y[:, rows, :])
 
         for c in range(2):
@@ -337,7 +339,7 @@ def tile_list_bilinear_flux_update_kernel(
             a_pair(2, jj)
         nc.vector.quantize_mx(out=wf_q[:].bitcast(FP8X4), scales=wf_sc[:], in_=wf_bf[:])
         quantize_h(0, 512)
-        flux(0, 512, (0, 1, 6, 7), (), 1)
+        flux(0, 512, (0, 1, 6, 7), (), (1, 2, 4))
         for jj in range(2):
             multiply_pair(2, jj)
             finish_fifth_group(jj)
@@ -349,10 +351,10 @@ def tile_list_bilinear_flux_update_kernel(
         finish_h(5)
         multiply_pair(3, 1)
         quantize_h(512, 256)
-        flux(512, 256, (4, 5), (), 2)
+        flux(512, 256, (4, 5), (), (2, 4))
         finish_h(6)
         finish_h(7)
         quantize_h(768, 128)
-        flux(768, 128, (1, 6), (2, 3), 4)
+        flux(768, 128, (1, 6), (2, 3), (4,))
         quantize_h(896, 128)
-        flux(896, 128, (7, 2), (2, 3), 4)
+        flux(896, 128, (7, 2), (2, 3), (4,))

@@ -20,7 +20,7 @@ IDENTITY = mybir.ActivationFunctionType.Identity
 
 P = 128
 HALF = 512
-AHEAD = 1024
+AHEAD = 2048
 
 
 def tile_list_bilinear_flux_update_kernel(

@@ -48,9 +48,9 @@ def tile_list_bilinear_flux_update_kernel(
         v_sc = tile("v_sc", [P, 2 * S], U8)
         wb_sc_raw = tile("wb_sc_raw", [P, 2, H], U8)
         wc_sc_raw = placed("wc_sc_raw", [P, 2, H], U8, 32)
-        wb_raw = placed("wb_raw", [P, 2, 2 * H], U8, 44)
-        wc_raw = placed("wc_raw", [P, 2, H], I32, 33)
-        wa_raw = [placed(f"wa_raw{a}", [P, 4, H], F32, 37 + 8 * a) for a in range(2)]
+        wb_raw = placed("wb_raw", [P, 2, 2 * H], U8, 50)
+        wc_raw = placed("wc_raw", [P, 2, H], I32, 51)
+        wa_raw = [placed(f"wa_raw{a}", [P, 4, H], F32, 34 + 9 * a) for a in range(2)]
         bias_rows = tile("bias_rows", [P, P], F32)
         identity = tile("identity", [P, P], F32)
         bias = tile("bias", [P, 8], F32)
@@ -104,7 +104,7 @@ def tile_list_bilinear_flux_update_kernel(
             )
         nc.vector.memset(wc_sc_raw[:].bitcast(I32), 0)
         load_words(1, AHEAD, T)
-        nc.sync.dma_start(out=wc_raw[:], in_=wc_words.rearrange("a p n i -> p a (n i)").bitcast(I32))
+        nc.sync.dma_start(out=wa_raw[0][:], in_=wa_rows[0])
         load_w_scales(wc_sc_raw, wc_scales, 4)
 
         wb_q = tile("wb_q", [P, 2, 2 * H], U8)
@@ -119,8 +119,8 @@ def tile_list_bilinear_flux_update_kernel(
         for q in range(4):
             deal(w_sc[0][32 * q : 32 * q + 4], wb_sc_raw[32 * q : 32 * q + 4], 2)
         deal(wb_q[:], wb_raw[:], 4)
-        for a in range(2):
-            nc.sync.dma_start(out=wa_raw[a][:], in_=wa_rows[a])
+        nc.sync.dma_start(out=wa_raw[1][:], in_=wa_rows[1])
+        nc.sync.dma_start(out=wc_raw[:], in_=wc_words.rearrange("a p n i -> p a (n i)").bitcast(I32))
         gather_words(0, 0)
         gather_words(0, 1)
 
@@ -140,7 +140,10 @@ def tile_list_bilinear_flux_update_kernel(
             for j in range(4):
                 b_pass(0, h, j)
 
-        b_sb = [[tile(f"b_sb{h}{jj}", [P, 2, HALF], F32) for jj in range(2)] for h in range(2)]
+        b_sb = [
+            [tile(f"b_sb0{jj}", [P, 2, HALF], F32) for jj in range(2)],
+            [placed(f"b_sb1{jj}", [P, 2, HALF], F32, 43 + 4 * jj) for jj in range(2)],
+        ]
 
         def add_background(h, j):
             nc.scalar.activation(
@@ -151,18 +154,16 @@ def tile_list_bilinear_flux_update_kernel(
             gather_words(1, h)
             for j in range(4):
                 b_pass(1, h, j)
-                add_background(h, j)
+        for j in range(4):
+            add_background(0, j)
 
         wf_raw = placed("wf_raw", [P, 4, N], F32, 0)
         wf_rows = wf.rearrange("(g t e) n -> t g e n", t=4, e=8)
         for t in range(4):
             nc.sync.dma_start(out=wf_raw[:, t, :], in_=wf_rows[t])
 
-        deal(wc_q[:], wc_raw[:], 8)
-        deal(w_sc[1][:], wc_sc_raw[:], 2)
-
-        c_bank = (0, 1, 2, 3, 4, 5, 3, 0)
-        a_bank = ((4, 5), (6, 7), (2, 3), (4, 2))
+        c_bank = (4, 5, 6, 7, 6, 7, 0, 2)
+        a_bank = ((0, 1), (2, 3), (0, 2), (1, 3))
 
         def c_group(g):
             h, n0 = divmod(128 * g, HALF)
@@ -178,24 +179,6 @@ def tile_list_bilinear_flux_update_kernel(
                         stop=(a == 1),
                     )
 
-        c_sb = tile("c_sb", [P, 2, 256, 2], F32)
-        for jj in range(2):
-            for e in range(2):
-                j = 2 * jj + e
-                for a in range(2):
-                    nc.tensor.matmul_mx(
-                        out=bank[jj][:, 256 * e : 256 * (e + 1)],
-                        lhsT=wc_q[:, a, 128 * j : 128 * (j + 1)].bitcast(FP8X4),
-                        lhsT_scale=w_sc[1][4:P, a, 128 * j : 128 * (j + 1)],
-                        rhs=v[a][0][:, 0:256].bitcast(FP8X4),
-                        rhs_scale=v_plane(a, slice(0, 256)),
-                        start=(a == 0),
-                        stop=(a == 1),
-                    )
-            nc.scalar.copy(c_sb[:, jj], bank[jj][:].rearrange("p (e n) -> p n e", e=2))
-        for g in range(2, 4):
-            c_group(g)
-
         wa_bf = [tile(f"wa_bf{a}", [P, 4 * H], BF16) for a in range(2)]
         wa_q = [tile(f"wa_q{a}", [P, H], U32) for a in range(2)]
         wa_sc = [tile(f"wa_sc{a}", [P, H], U8) for a in range(2)]
@@ -209,8 +192,8 @@ def tile_list_bilinear_flux_update_kernel(
                 lhsT_scale=wa_sc[a][:, 128 * j : 128 * (j + 1)],
                 rhs=v[a][h][:, m0 : m0 + n].bitcast(FP8X4),
                 rhs_scale=v_plane(a, slice(n0, n0 + n)),
-                start=(a == (0 if c == 0 else 1) and j % 2 == 0),
-                stop=(a == (1 if c == 0 else 0) and j % 2 == 1),
+                start=(a == 0 and j % 2 == 0),
+                stop=(a == 1 and j % 2 == 1),
             )
 
         wa_dst = [wa_bf[a][:].rearrange("p (t g f e j) -> p t g f j e", t=4, f=2, e=4, j=4) for a in range(2)]
@@ -218,32 +201,42 @@ def tile_list_bilinear_flux_update_kernel(
         for t in range(4):
             nc.vector.tensor_copy(wa_dst[0][:, t], wa_src[0][:, t])
         nc.vector.quantize_mx(out=wa_q[0][:].bitcast(FP8X4), scales=wa_sc[0][:], in_=wa_bf[0][:])
+        deal(w_sc[1][:], wc_sc_raw[:], 2)
 
+        for c in range(2):
+            for j in range(4):
+                a_pass(c, 0, j)
+
+        def quantize_wa(j):
+            nc.vector.quantize_mx(
+                out=wa_q[1][:, 128 * j : 128 * (j + 1)].bitcast(FP8X4),
+                scales=wa_sc[1][:, 128 * j : 128 * (j + 1)],
+                in_=wa_bf[1][:, 512 * j : 512 * (j + 1)],
+            )
+
+        for t in range(2):
+            nc.vector.tensor_copy(wa_dst[1][:, t], wa_src[1][:, t])
+            nc.scalar.copy(wa_dst[1][:, 2 + t], wa_src[1][:, 2 + t])
         for j in range(4):
-            a_pass(0, 0, j)
-
-        for js in ((0, 1, 2), (3,)):
-            for j in js:
-                nc.vector.tensor_copy(wa_dst[1][:, j % 3], wa_src[1][:, j])
-            for j in (0, 1) if 0 in js else (2, 3):
-                nc.vector.quantize_mx(
-                    out=wa_q[1][:, 128 * j : 128 * (j + 1)].bitcast(FP8X4),
-                    scales=wa_sc[1][:, 128 * j : 128 * (j + 1)],
-                    in_=wa_bf[1][:, 512 * (j % 3) : 512 * (j % 3 + 1)],
-                )
+            add_background(1, j)
+        quantize_wa(0)
+        quantize_wa(1)
+        deal(wc_q[:], wc_raw[:], 8)
+        quantize_wa(2)
+        quantize_wa(3)
 
         def a_pair(c, jj):
-            for a in (1,) if c == 0 else (1, 0):
+            for a in (1,) if c < 2 else (0, 1):
                 for j in (2 * jj, 2 * jj + 1):
                     a_pass(c, a, j)
 
         ab = [tile(f"ab{c}", [P, 2, 256, 2], F32) for c in range(4)]
 
-        def multiply_pair(c, jj, n0=0, n=256):
-            cols = slice(256 * (c % 2) + n0, 256 * (c % 2) + n0 + n)
+        def multiply_pair(c, jj):
+            cols = slice(256 * (c % 2), 256 * (c % 2 + 1))
             nc.vector.tensor_tensor(
-                ab[c][:, jj, n0 : n0 + n],
-                bank[a_bank[c][jj]][:].rearrange("p (e n) -> p n e", e=2)[:, n0 : n0 + n],
+                ab[c][:, jj],
+                bank[a_bank[c][jj]][:].rearrange("p (e n) -> p n e", e=2),
                 b_sb[c // 2][jj][:, :, cols].rearrange("p e n -> p n e"),
                 MULT,
             )
@@ -267,21 +260,6 @@ def tile_list_bilinear_flux_update_kernel(
                 h_bf[:, 512 * g : 512 * (g + 1)].rearrange("p (n jj e) -> p n jj e", jj=2, e=2),
                 bank[c_bank[g]][:].rearrange("p (jj e n) -> p n jj e", jj=2, e=2),
                 ab[g // 2][:, :, n0 : n0 + 128, :].rearrange("p jj n e -> p n jj e"),
-                ADD,
-            )
-
-        def finish_first_chunk(jj):
-            nc.gpsimd.tensor_tensor(
-                h_bf[:, 0:1024].rearrange("p (n jj e) -> p jj n e", jj=2, e=2)[:, jj], ab[0][:, jj], c_sb[:, jj], ADD
-            )
-
-        c4_sb = tile("c4_sb", [P, 2, 128, 2], F32)
-
-        def finish_fifth_group(jj):
-            nc.gpsimd.tensor_tensor(
-                h_bf[:, 2048:2560].rearrange("p (n jj e) -> p jj n e", jj=2, e=2)[:, jj],
-                ab[2][:, jj, 0:128],
-                c4_sb[:, jj],
                 ADD,
             )
 
@@ -321,33 +299,33 @@ def tile_list_bilinear_flux_update_kernel(
                     rows = slice(max([0] + [end for end in stores if end <= t]), t + 1)
                     nc.sync.dma_start(out=out_rows[:, rows, n0 : n0 + n], in_=y[:, rows, :])
 
-        for c in range(2):
+        for jj in range(2):
+            for c in range(2):
+                a_pair(c, jj)
+        for g in range(4):
+            c_group(g)
+        for jj in range(2):
+            for c in range(2):
+                multiply_pair(c, jj)
+        for c in range(2, 4):
             for jj in range(2):
                 a_pair(c, jj)
-        for jj in range(2):
-            multiply_pair(0, jj)
-            finish_first_chunk(jj)
-        c_group(4)
-        nc.scalar.copy(c4_sb[:], bank[c_bank[4]][:].rearrange("p (jj e n) -> p jj n e", jj=2, e=2))
-        c_group(5)
-        multiply_pair(1, 0)
-        multiply_pair(1, 1, 0, 128)
-        multiply_pair(1, 1, 128, 128)
-        finish_h(2)
-        finish_h(3)
-        for jj in range(2):
-            a_pair(2, jj)
+        for g in range(3):
+            finish_h(g)
         nc.vector.quantize_mx(out=wf_q[:].bitcast(FP8X4), scales=wf_sc[:], in_=wf_bf[:])
-        quantize_h(0, 512)
-        flux(0, 512, (0, 1, 6, 7), (), (1, 2, 4))
-        for jj in range(2):
-            multiply_pair(2, jj)
-            finish_fifth_group(jj)
-        for jj in range(2):
-            a_pair(3, jj)
+        quantize_h(0, 256)
+        flux(0, 256, (4, 5), (), (4,))
+        c_group(4)
+        finish_h(3)
+        c_group(5)
+        multiply_pair(2, 0)
+        quantize_h(256, 256)
+        flux(256, 256, (4, 5), (), (2, 4))
         c_group(6)
+        multiply_pair(2, 1)
         c_group(7)
         multiply_pair(3, 0)
+        finish_h(4)
         finish_h(5)
         multiply_pair(3, 1)
         quantize_h(512, 256)
@@ -357,4 +335,4 @@ def tile_list_bilinear_flux_update_kernel(
         quantize_h(768, 128)
         flux(768, 128, (1, 6), (2, 3), (4,))
         quantize_h(896, 128)
-        flux(896, 128, (7, 2), (2, 3), (4,))
+        flux(896, 128, (7, 3), (2, 3), (4,))

@@ -46,8 +46,7 @@ def tile_list_bilinear_flux_update_kernel(
         table_sc = placed("table_sc", [P, T], U8, 31)
         picked_sc = tile("picked_sc", [P, S], U8)
         v_sc = tile("v_sc", [P, 2 * S], U8)
-        wb_sc_raw = tile("wb_sc_raw", [P, 2, H], U8)
-        wc_sc_raw = placed("wc_sc_raw", [P, 2, H], U8, 32)
+        w_sc_raw = tile("w_sc_raw", [P, 2, H], U8)
         wb_raw = placed("wb_raw", [P, 2, 2 * H], U8, 50)
         wc_raw = placed("wc_raw", [P, 2, H], I32, 51)
         wa_raw = [placed(f"wa_raw{a}", [P, 4, H], F32, 34 + 9 * a) for a in range(2)]
@@ -57,8 +56,8 @@ def tile_list_bilinear_flux_update_kernel(
 
         nc.vector.memset(table_sc[32:64, :].bitcast(I32), 0)
         nc.vector.memset(table_sc[64:P, :].bitcast(I32), 0)
-        w_sc = [tile("wb_sc", [P, 2, H], U8), tile("wc_sc", [P, 2, H], U8)]
-        nc.vector.memset(w_sc[0][:].bitcast(I32), 0)
+        w_sc = tile("w_sc", [P, 2, H], U8)
+        nc.vector.memset(w_sc[:].bitcast(I32), 0)
         nc.vector.memset(v_sc[:].bitcast(I32), 0)
 
         def load_words(a, t0, t1):
@@ -76,8 +75,9 @@ def tile_list_bilinear_flux_update_kernel(
         nc.sync.dma_start(offsets[:], offs)
         nc.sync.dma_start(out=table_sc[0:32, :].bitcast(I32), in_=tab_scales.rearrange("a q t -> q a t").bitcast(I32))
         nc.sync.dma_start(out=wb_raw[:].bitcast(I32), in_=wb_words.rearrange("a p n -> p a n").bitcast(I32))
-        load_w_scales(wb_sc_raw, wb_scales, 0)
+        load_w_scales(w_sc_raw, wb_scales, 0)
         load_words(0, 0, T)
+        load_w_scales(w_sc_raw, wc_scales, 4)
         load_words(1, 0, AHEAD)
 
         nc.gpsimd.memset(bias_rows[:], 0.0)
@@ -102,10 +102,8 @@ def tile_list_bilinear_flux_update_kernel(
             nc.sync.dma_start(
                 out=v_sc[32 * q : 32 * q + 4, :].bitcast(I32), in_=picked_sc[8 * q : 8 * q + 8, :].bitcast(I32)
             )
-        nc.vector.memset(wc_sc_raw[:].bitcast(I32), 0)
         load_words(1, AHEAD, T)
         nc.sync.dma_start(out=wa_raw[0][:], in_=wa_rows[0])
-        load_w_scales(wc_sc_raw, wc_scales, 4)
 
         wb_q = tile("wb_q", [P, 2, 2 * H], U8)
         wc_q = tile("wc_q", [P, 2, H], U32)
@@ -116,9 +114,9 @@ def tile_list_bilinear_flux_update_kernel(
                 src.bitcast(I32).rearrange("p a (g t e) -> p a t g e", t=4, e=words),
             )
 
-        for q in range(4):
-            deal(w_sc[0][32 * q : 32 * q + 4], wb_sc_raw[32 * q : 32 * q + 4], 2)
         deal(wb_q[:], wb_raw[:], 4)
+        for q in range(4):
+            deal(w_sc[32 * q : 32 * q + 8], w_sc_raw[32 * q : 32 * q + 8], 2)
         nc.sync.dma_start(out=wa_raw[1][:], in_=wa_rows[1])
         nc.sync.dma_start(out=wc_raw[:], in_=wc_words.rearrange("a p n i -> p a (n i)").bitcast(I32))
         gather_words(0, 0)
@@ -129,7 +127,7 @@ def tile_list_bilinear_flux_update_kernel(
             nc.tensor.matmul_mx(
                 out=bank[4 * h + j][:],
                 lhsT=wb_q[:, a, 256 * j : 256 * (j + 1)].bitcast(FP4X4),
-                lhsT_scale=w_sc[0][:, a, 128 * j : 128 * (j + 1)],
+                lhsT_scale=w_sc[:, a, 128 * j : 128 * (j + 1)],
                 rhs=v[a][h][:].bitcast(FP8X4),
                 rhs_scale=v_plane(a, cols),
                 start=(a == 0),
@@ -162,8 +160,8 @@ def tile_list_bilinear_flux_update_kernel(
         for t in range(4):
             nc.sync.dma_start(out=wf_raw[:, t, :], in_=wf_rows[t])
 
-        c_bank = (4, 5, 6, 7, 6, 7, 0, 2)
-        a_bank = ((0, 1), (2, 3), (0, 2), (1, 3))
+        c_bank = (4, 5, 6, 0, 5, 6, 5, 6)
+        a_bank = ((0, 1), (2, 3), (2, 4), (1, 3))
 
         def c_group(g):
             h, n0 = divmod(128 * g, HALF)
@@ -172,7 +170,7 @@ def tile_list_bilinear_flux_update_kernel(
                     nc.tensor.matmul_mx(
                         out=bank[c_bank[g]][:, 128 * j : 128 * (j + 1)],
                         lhsT=wc_q[:, a, 128 * j : 128 * (j + 1)].bitcast(FP8X4),
-                        lhsT_scale=w_sc[1][4:P, a, 128 * j : 128 * (j + 1)],
+                        lhsT_scale=w_sc[4:P, a, 128 * j : 128 * (j + 1)],
                         rhs=v[a][h][:, n0 : n0 + 128].bitcast(FP8X4),
                         rhs_scale=v_plane(a, slice(128 * g, 128 * (g + 1))),
                         start=(a == 0),
@@ -201,7 +199,6 @@ def tile_list_bilinear_flux_update_kernel(
         for t in range(4):
             nc.vector.tensor_copy(wa_dst[0][:, t], wa_src[0][:, t])
         nc.vector.quantize_mx(out=wa_q[0][:].bitcast(FP8X4), scales=wa_sc[0][:], in_=wa_bf[0][:])
-        deal(w_sc[1][:], wc_sc_raw[:], 2)
 
         for c in range(2):
             for j in range(4):
@@ -217,7 +214,7 @@ def tile_list_bilinear_flux_update_kernel(
         for t in range(2):
             nc.vector.tensor_copy(wa_dst[1][:, t], wa_src[1][:, t])
             nc.scalar.copy(wa_dst[1][:, 2 + t], wa_src[1][:, 2 + t])
-        for j in range(4):
+        for j in range(2):
             add_background(1, j)
         quantize_wa(0)
         quantize_wa(1)
@@ -232,11 +229,11 @@ def tile_list_bilinear_flux_update_kernel(
 
         ab = [tile(f"ab{c}", [P, 2, 256, 2], F32) for c in range(4)]
 
-        def multiply_pair(c, jj):
-            cols = slice(256 * (c % 2), 256 * (c % 2 + 1))
+        def multiply_pair(c, jj, n0=0, n=256):
+            cols = slice(256 * (c % 2) + n0, 256 * (c % 2) + n0 + n)
             nc.vector.tensor_tensor(
-                ab[c][:, jj],
-                bank[a_bank[c][jj]][:].rearrange("p (e n) -> p n e", e=2),
+                ab[c][:, jj, n0 : n0 + n],
+                bank[a_bank[c][jj]][:].rearrange("p (e n) -> p n e", e=2)[:, n0 : n0 + n],
                 b_sb[c // 2][jj][:, :, cols].rearrange("p e n -> p n e"),
                 MULT,
             )
@@ -246,8 +243,6 @@ def tile_list_bilinear_flux_update_kernel(
         wf_sc = tile("wf_sc", [P, N], U8)
         wf_dst = wf_bf[:].rearrange("p (c i j) -> p c j i", i=4, j=4)
         wf_src = wf_raw[:].rearrange("p j (c i) -> p c j i", i=4)
-        for s in range(2):
-            nc.scalar.copy(wf_dst[:, 64 * s : 64 * (s + 1)], wf_src[:, 64 * s : 64 * (s + 1)])
 
         h_bf = tile("h_bf", [P, 4 * S], BF16)
         h_q = tile("h_q", [P, S], U32)
@@ -289,8 +284,8 @@ def tile_list_bilinear_flux_update_kernel(
 
         def flux(n0, n, banks, vector_share, stores):
             y = tile(f"y{n0}", [P, 4, n], F32)
-            per_bank = 4 // len(banks)
-            sums = [bank[banks[t // per_bank]][:, (t % per_bank) * n : (t % per_bank + 1) * n] for t in range(4)]
+            place = [len([b for b in banks[:t] if b == banks[t]]) for t in range(4)]
+            sums = [bank[banks[t]][:, place[t] * n : (place[t] + 1) * n] for t in range(4)]
             for t in range(4):
                 flux_pass(sums[t], t, n0, n)
             for t in range(4):
@@ -299,40 +294,60 @@ def tile_list_bilinear_flux_update_kernel(
                     rows = slice(max([0] + [end for end in stores if end <= t]), t + 1)
                     nc.sync.dma_start(out=out_rows[:, rows, n0 : n0 + n], in_=y[:, rows, :])
 
+        c_sb = tile("c_sb", [P, 2, 128, 2], F32)
+
+        def finish_first_group(jj):
+            nc.gpsimd.tensor_tensor(
+                h_bf[:, 0:512].rearrange("p (n jj e) -> p jj n e", jj=2, e=2)[:, jj],
+                ab[0][:, jj, 0:128],
+                c_sb[:, jj],
+                ADD,
+            )
+
         for jj in range(2):
             for c in range(2):
                 a_pair(c, jj)
-        for g in range(4):
-            c_group(g)
+        c_group(0)
+        nc.scalar.copy(c_sb[:], bank[c_bank[0]][:].rearrange("p (jj e n) -> p jj n e", jj=2, e=2))
+        for s in range(2):
+            nc.scalar.copy(wf_dst[:, 64 * s : 64 * (s + 1)], wf_src[:, 64 * s : 64 * (s + 1)])
+        for j in range(2, 4):
+            add_background(1, j)
+        c_group(1)
+        c_group(2)
+        multiply_pair(0, 0)
+        finish_first_group(0)
+        c_group(3)
+        multiply_pair(1, 0)
+        multiply_pair(0, 1)
+        finish_first_group(1)
+        multiply_pair(1, 1)
         for jj in range(2):
-            for c in range(2):
-                multiply_pair(c, jj)
-        for c in range(2, 4):
-            for jj in range(2):
-                a_pair(c, jj)
-        for g in range(3):
-            finish_h(g)
-        nc.vector.quantize_mx(out=wf_q[:].bitcast(FP8X4), scales=wf_sc[:], in_=wf_bf[:])
-        quantize_h(0, 256)
-        flux(0, 256, (4, 5), (), (4,))
+            a_pair(2, jj)
+        finish_h(1)
         c_group(4)
-        finish_h(3)
+        finish_h(2)
         c_group(5)
+        finish_h(3)
+        a_pair(3, 0)
         multiply_pair(2, 0)
-        quantize_h(256, 256)
-        flux(256, 256, (4, 5), (), (2, 4))
-        c_group(6)
+        nc.vector.quantize_mx(out=wf_q[:].bitcast(FP8X4), scales=wf_sc[:], in_=wf_bf[:])
+        quantize_h(0, 512)
         multiply_pair(2, 1)
-        c_group(7)
+        flux(0, 512, (0, 2, 7, 4), (), (1, 2, 4))
+        a_pair(3, 1)
         multiply_pair(3, 0)
         finish_h(4)
+        c_group(6)
         finish_h(5)
-        multiply_pair(3, 1)
+        multiply_pair(3, 1, 0, 128)
         quantize_h(512, 256)
-        flux(512, 256, (4, 5), (), (2, 4))
+        flux(512, 256, (1, 1, 0, 0), (), (2, 4))
+        c_group(7)
         finish_h(6)
-        finish_h(7)
+        multiply_pair(3, 1, 128, 128)
         quantize_h(768, 128)
-        flux(768, 128, (1, 6), (2, 3), (4,))
+        finish_h(7)
+        flux(768, 128, (2, 2, 2, 3), (3,), (4,))
         quantize_h(896, 128)
-        flux(896, 128, (7, 3), (2, 3), (4,))
+        flux(896, 128, (5, 5, 7, 7), (2, 3), (4,))

@@ -34,10 +34,10 @@ def tile_list_bilinear_flux_update_kernel(
         psum = ctx.enter_context(tc.psum_pool(name="psum", bufs=1))
 
         def tile(name, shape, dtype):
-            return sb.tile(shape, dtype, name=name, align_bytes=64)
+            return sb.tile(shape, dtype, name=name, align_bytes=256)
 
         def placed(name, shape, dtype, kib):
-            return shared.tile(shape, dtype, name=name, align_bytes=64, offset=1024 * kib)
+            return shared.tile(shape, dtype, name=name, align_bytes=256, offset=1024 * kib)
 
         bank = [psum.tile([P, 512], F32, name=f"bank{i}") for i in range(8)]
 

@@ -36,6 +36,9 @@ def tile_list_bilinear_flux_update_kernel(
         def tile(name, shape, dtype):
             return sb.tile(shape, dtype, name=name, align_bytes=256)
 
+        def shifted(name, words):
+            return tile(name, [P, words + 32], U32)[:, 32:]
+
         def placed(name, shape, dtype, kib):
             return shared.tile(shape, dtype, name=name, align_bytes=256, offset=1024 * kib)
 
@@ -105,8 +108,8 @@ def tile_list_bilinear_flux_update_kernel(
         load_words(1, AHEAD, T)
         nc.sync.dma_start(out=wa_raw[0][:], in_=wa_rows[0])
 
-        wb_q = tile("wb_q", [P, 2, 2 * H], U8)
-        wc_q = tile("wc_q", [P, 2, H], U32)
+        wb_q = shifted("wb_q", H).bitcast(U8).rearrange("p (a n) -> p a n", a=2)
+        wc_q = shifted("wc_q", 2 * H).rearrange("p (a n) -> p a n", a=2)
 
         def deal(dst, src, words):
             nc.vector.tensor_copy(
@@ -178,7 +181,7 @@ def tile_list_bilinear_flux_update_kernel(
                     )
 
         wa_bf = [tile(f"wa_bf{a}", [P, 4 * H], BF16) for a in range(2)]
-        wa_q = [tile(f"wa_q{a}", [P, H], U32) for a in range(2)]
+        wa_q = [shifted(f"wa_q{a}", H) for a in range(2)]
         wa_sc = [tile(f"wa_sc{a}", [P, H], U8) for a in range(2)]
 
         def a_pass(c, a, j):
@@ -239,7 +242,7 @@ def tile_list_bilinear_flux_update_kernel(
             )
 
         wf_bf = tile("wf_bf", [P, 4 * N], BF16)
-        wf_q = tile("wf_q", [P, N], U32)
+        wf_q = shifted("wf_q", N)
         wf_sc = tile("wf_sc", [P, N], U8)
         wf_dst = wf_bf[:].rearrange("p (c i j) -> p c j i", i=4, j=4)
         wf_src = wf_raw[:].rearrange("p j (c i) -> p c j i", i=4)

@@ -60,8 +60,6 @@ def tile_list_bilinear_flux_update_kernel(
         nc.vector.memset(table_sc[32:64, :].bitcast(I32), 0)
         nc.vector.memset(table_sc[64:P, :].bitcast(I32), 0)
         w_sc = tile("w_sc", [P, 2, H], U8)
-        nc.vector.memset(w_sc[:].bitcast(I32), 0)
-        nc.vector.memset(v_sc[:].bitcast(I32), 0)
 
         def load_words(a, t0, t1):
             words = tab_words[a].rearrange("p t i -> p (t i)").bitcast(I32)
@@ -89,6 +87,8 @@ def tile_list_bilinear_flux_update_kernel(
         )
         nc.gpsimd.dma_start(out=bias_rows[4:8, :], in_=bf.rearrange("(t m) -> t m", t=4))
         make_identity(nc, identity[:])
+        nc.gpsimd.memset(v_sc[:].bitcast(I32), 0)
+        nc.gpsimd.memset(w_sc[:].bitcast(I32), 0)
         nc.tensor.transpose(bank[7][:, 0:P], bias_rows[:], identity[:])
         nc.scalar.copy(bias[:], bank[7][:, 0:8])
 
@@ -111,15 +111,15 @@ def tile_list_bilinear_flux_update_kernel(
         wb_q = shifted("wb_q", H).bitcast(U8).rearrange("p (a n) -> p a n", a=2)
         wc_q = shifted("wc_q", 2 * H).rearrange("p (a n) -> p a n", a=2)
 
-        def deal(dst, src, words):
-            nc.vector.tensor_copy(
+        def deal(engine, dst, src, words):
+            engine.tensor_copy(
                 dst.bitcast(I32).rearrange("p a (t g e) -> p a t g e", t=4, e=words),
                 src.bitcast(I32).rearrange("p a (g t e) -> p a t g e", t=4, e=words),
             )
 
-        deal(wb_q[:], wb_raw[:], 4)
+        deal(nc.vector, wb_q[:], wb_raw[:], 4)
         for q in range(4):
-            deal(w_sc[32 * q : 32 * q + 8], w_sc_raw[32 * q : 32 * q + 8], 2)
+            deal(nc.gpsimd, w_sc[32 * q : 32 * q + 8], w_sc_raw[32 * q : 32 * q + 8], 2)
         nc.sync.dma_start(out=wa_raw[1][:], in_=wa_rows[1])
         nc.sync.dma_start(out=wc_raw[:], in_=wc_words.rearrange("a p n i -> p a (n i)").bitcast(I32))
         gather_words(0, 0)
@@ -207,11 +207,11 @@ def tile_list_bilinear_flux_update_kernel(
             for j in range(4):
                 a_pass(c, 0, j)
 
-        def quantize_wa(j):
+        def quantize_wa(j, tiles):
             nc.vector.quantize_mx(
-                out=wa_q[1][:, 128 * j : 128 * (j + 1)].bitcast(FP8X4),
-                scales=wa_sc[1][:, 128 * j : 128 * (j + 1)],
-                in_=wa_bf[1][:, 512 * j : 512 * (j + 1)],
+                out=wa_q[1][:, 128 * j : 128 * (j + tiles)].bitcast(FP8X4),
+                scales=wa_sc[1][:, 128 * j : 128 * (j + tiles)],
+                in_=wa_bf[1][:, 512 * j : 512 * (j + tiles)],
             )
 
         for t in range(2):
@@ -219,11 +219,11 @@ def tile_list_bilinear_flux_update_kernel(
             nc.scalar.copy(wa_dst[1][:, 2 + t], wa_src[1][:, 2 + t])
         for j in range(2):
             add_background(1, j)
-        quantize_wa(0)
-        quantize_wa(1)
-        deal(wc_q[:], wc_raw[:], 8)
-        quantize_wa(2)
-        quantize_wa(3)
+        quantize_wa(0, 1)
+        quantize_wa(1, 1)
+        deal(nc.vector, wc_q[:], wc_raw[:], 8)
+        quantize_wa(2, 1)
+        quantize_wa(3, 1)
 
         def a_pair(c, jj):
             for a in (1,) if c < 2 else (0, 1):

@@ -199,31 +199,34 @@ def tile_list_bilinear_flux_update_kernel(
 
         wa_dst = [wa_bf[a][:].rearrange("p (t g f e j) -> p t g f j e", t=4, f=2, e=4, j=4) for a in range(2)]
         wa_src = [wa_raw[a][:].rearrange("p j (g t f e) -> p t g f j e", t=4, f=2, e=4) for a in range(2)]
-        for t in range(4):
-            nc.vector.tensor_copy(wa_dst[0][:, t], wa_src[0][:, t])
-        nc.vector.quantize_mx(out=wa_q[0][:].bitcast(FP8X4), scales=wa_sc[0][:], in_=wa_bf[0][:])
 
-        for c in range(2):
-            for j in range(4):
-                a_pass(c, 0, j)
-
-        def quantize_wa(j, tiles):
+        def quantize_wa(a, j, tiles):
             nc.vector.quantize_mx(
-                out=wa_q[1][:, 128 * j : 128 * (j + tiles)].bitcast(FP8X4),
-                scales=wa_sc[1][:, 128 * j : 128 * (j + tiles)],
-                in_=wa_bf[1][:, 512 * j : 512 * (j + tiles)],
+                out=wa_q[a][:, 128 * j : 128 * (j + tiles)].bitcast(FP8X4),
+                scales=wa_sc[a][:, 128 * j : 128 * (j + tiles)],
+                in_=wa_bf[a][:, 512 * j : 512 * (j + tiles)],
             )
+
+        for t in range(3):
+            nc.vector.tensor_copy(wa_dst[0][:, t], wa_src[0][:, t])
+        quantize_wa(0, 0, 2)
+        nc.vector.tensor_copy(wa_dst[0][:, 3], wa_src[0][:, 3])
+        quantize_wa(0, 2, 2)
+        for jj in range(2):
+            for c in range(2):
+                for j in (2 * jj, 2 * jj + 1):
+                    a_pass(c, 0, j)
 
         for t in range(2):
             nc.vector.tensor_copy(wa_dst[1][:, t], wa_src[1][:, t])
             nc.scalar.copy(wa_dst[1][:, 2 + t], wa_src[1][:, 2 + t])
         for j in range(2):
             add_background(1, j)
-        quantize_wa(0, 1)
-        quantize_wa(1, 1)
+        quantize_wa(1, 0, 1)
+        quantize_wa(1, 1, 1)
         deal(nc.vector, wc_q[:], wc_raw[:], 8)
-        quantize_wa(2, 1)
-        quantize_wa(3, 1)
+        quantize_wa(1, 2, 1)
+        quantize_wa(1, 3, 1)
 
         def a_pair(c, jj):
             for a in (1,) if c < 2 else (0, 1):
@@ -247,7 +250,7 @@ def tile_list_bilinear_flux_update_kernel(
         wf_dst = wf_bf[:].rearrange("p (c i j) -> p c j i", i=4, j=4)
         wf_src = wf_raw[:].rearrange("p j (c i) -> p c j i", i=4)
 
-        h_bf = tile("h_bf", [P, 4 * S], BF16)
+        h_bf = tile("h_bf", [P, 4 * HALF], BF16)
         h_q = tile("h_q", [P, S], U32)
         h_sc = tile("h_sc", [P, S], U8)
         out_rows = out.rearrange("(t p) s -> p t s", p=P)
@@ -255,7 +258,7 @@ def tile_list_bilinear_flux_update_kernel(
         def finish_h(g):
             n0 = 128 * (g % 2)
             nc.vector.tensor_tensor(
-                h_bf[:, 512 * g : 512 * (g + 1)].rearrange("p (n jj e) -> p n jj e", jj=2, e=2),
+                h_bf[:, 512 * (g % 4) : 512 * (g % 4 + 1)].rearrange("p (n jj e) -> p n jj e", jj=2, e=2),
                 bank[c_bank[g]][:].rearrange("p (jj e n) -> p n jj e", jj=2, e=2),
                 ab[g // 2][:, :, n0 : n0 + 128, :].rearrange("p jj n e -> p n jj e"),
                 ADD,
@@ -265,7 +268,7 @@ def tile_list_bilinear_flux_update_kernel(
             nc.vector.quantize_mx(
                 out=h_q[:, n0 : n0 + n].bitcast(FP8X4),
                 scales=h_sc[:, n0 : n0 + n],
-                in_=h_bf[:, 4 * n0 : 4 * (n0 + n)],
+                in_=h_bf[:, 4 * (n0 % HALF) : 4 * (n0 % HALF + n)],
             )
 
         def flux_pass(dst, t, n0, n):
@@ -285,25 +288,35 @@ def tile_list_bilinear_flux_update_kernel(
             else:
                 nc.scalar.activation(dst, src, IDENTITY, bias=bias[:, 4 + t : 5 + t])
 
-        def flux(n0, n, banks, vector_share, stores):
+        results = {}
+
+        def flux(n0, n, banks):
             y = tile(f"y{n0}", [P, 4, n], F32)
             place = [len([b for b in banks[:t] if b == banks[t]]) for t in range(4)]
             sums = [bank[banks[t]][:, place[t] * n : (place[t] + 1) * n] for t in range(4)]
             for t in range(4):
                 flux_pass(sums[t], t, n0, n)
-            for t in range(4):
-                add_bias(y[:, t, :], sums[t], t, t in vector_share)
-                if t + 1 in stores:
-                    rows = slice(max([0] + [end for end in stores if end <= t]), t + 1)
-                    nc.sync.dma_start(out=out_rows[:, rows, n0 : n0 + n], in_=y[:, rows, :])
+            results[n0] = (n, y, sums)
 
-        c_sb = tile("c_sb", [P, 2, 128, 2], F32)
+        def finish_rows(n0, tiles, on_vector=False):
+            n, y, sums = results[n0]
+            for t in tiles:
+                add_bias(y[:, t, :], sums[t], t, on_vector)
 
-        def finish_first_group(jj):
+        def store(n0, t0, t1):
+            n, y, sums = results[n0]
+            nc.sync.dma_start(out=out_rows[:, t0:t1, n0 : n0 + n], in_=y[:, t0:t1, :])
+
+        c_sb = {g: tile(f"c_sb{g}", [P, 2, 128, 2], F32) for g in (0, 4)}
+
+        def copy_c(g):
+            nc.scalar.copy(c_sb[g][:], bank[c_bank[g]][:].rearrange("p (jj e n) -> p jj n e", jj=2, e=2))
+
+        def finish_on_gpsimd(g, jj):
             nc.gpsimd.tensor_tensor(
                 h_bf[:, 0:512].rearrange("p (n jj e) -> p jj n e", jj=2, e=2)[:, jj],
-                ab[0][:, jj, 0:128],
-                c_sb[:, jj],
+                ab[g // 2][:, jj, 0:128],
+                c_sb[g][:, jj],
                 ADD,
             )
 
@@ -311,7 +324,7 @@ def tile_list_bilinear_flux_update_kernel(
             for c in range(2):
                 a_pair(c, jj)
         c_group(0)
-        nc.scalar.copy(c_sb[:], bank[c_bank[0]][:].rearrange("p (jj e n) -> p jj n e", jj=2, e=2))
+        copy_c(0)
         for s in range(2):
             nc.scalar.copy(wf_dst[:, 64 * s : 64 * (s + 1)], wf_src[:, 64 * s : 64 * (s + 1)])
         for j in range(2, 4):
@@ -319,16 +332,17 @@ def tile_list_bilinear_flux_update_kernel(
         c_group(1)
         c_group(2)
         multiply_pair(0, 0)
-        finish_first_group(0)
+        finish_on_gpsimd(0, 0)
         c_group(3)
         multiply_pair(1, 0)
         multiply_pair(0, 1)
-        finish_first_group(1)
+        finish_on_gpsimd(0, 1)
         multiply_pair(1, 1)
         for jj in range(2):
             a_pair(2, jj)
         finish_h(1)
         c_group(4)
+        copy_c(4)
         finish_h(2)
         c_group(5)
         finish_h(3)
@@ -336,21 +350,36 @@ def tile_list_bilinear_flux_update_kernel(
         multiply_pair(2, 0)
         nc.vector.quantize_mx(out=wf_q[:].bitcast(FP8X4), scales=wf_sc[:], in_=wf_bf[:])
         quantize_h(0, 512)
+        finish_on_gpsimd(4, 0)
         multiply_pair(2, 1)
-        flux(0, 512, (0, 2, 7, 4), (), (1, 2, 4))
+        finish_on_gpsimd(4, 1)
+        flux(0, 512, (0, 2, 7, 4))
+        for t0, t1 in ((0, 1), (1, 2), (2, 4)):
+            finish_rows(0, range(t0, t1))
+            store(0, t0, t1)
         a_pair(3, 1)
-        multiply_pair(3, 0)
-        finish_h(4)
         c_group(6)
+        multiply_pair(3, 0)
         finish_h(5)
+        c_group(7)
         multiply_pair(3, 1, 0, 128)
         quantize_h(512, 256)
-        flux(512, 256, (1, 1, 0, 0), (), (2, 4))
-        c_group(7)
+        flux(512, 256, (1, 1, 0, 4))
+        finish_rows(512, (0, 1))
+        store(512, 0, 2)
+        finish_rows(512, (2,))
         finish_h(6)
         multiply_pair(3, 1, 128, 128)
         quantize_h(768, 128)
         finish_h(7)
-        flux(768, 128, (2, 2, 2, 3), (3,), (4,))
+        finish_rows(512, (3,), True)
+        store(512, 2, 4)
         quantize_h(896, 128)
-        flux(896, 128, (5, 5, 7, 7), (2, 3), (4,))
+        flux(768, 128, (2, 2, 2, 3))
+        finish_rows(768, (0, 1, 2))
+        finish_rows(768, (3,), True)
+        store(768, 0, 4)
+        flux(896, 128, (5, 5, 7, 7))
+        finish_rows(896, (0, 1))
+        finish_rows(896, (2, 3), True)
+        store(896, 0, 4)

@@ -176,8 +176,8 @@ def tile_list_bilinear_flux_update_kernel(
                         lhsT_scale=w_sc[4:P, a, 128 * j : 128 * (j + 1)],
                         rhs=v[a][h][:, n0 : n0 + 128].bitcast(FP8X4),
                         rhs_scale=v_plane(a, slice(128 * g, 128 * (g + 1))),
-                        start=(a == 0),
-                        stop=(a == 1),
+                        start=(a == 0 and j == 0),
+                        stop=(a == 1 and j == 3),
                     )
 
         wa_bf = [tile(f"wa_bf{a}", [P, 4 * H], BF16) for a in range(2)]
@@ -375,9 +375,9 @@ def tile_list_bilinear_flux_update_kernel(
         finish_rows(512, (3,), True)
         store(512, 2, 4)
         quantize_h(896, 128)
-        flux(768, 128, (2, 2, 2, 3))
-        finish_rows(768, (0, 1, 2))
-        finish_rows(768, (3,), True)
+        flux(768, 128, (2, 2, 3, 3))
+        finish_rows(768, (0, 1))
+        finish_rows(768, (2, 3), True)
         store(768, 0, 4)
         flux(896, 128, (5, 5, 7, 7))
         finish_rows(896, (0, 1))

from contextlib import ExitStack

import concourse.mybir as mybir
from concourse.masks import make_identity

K, T, S, H, N = 1024, 4096, 1024, 512, 512
FLOPS = 2 * S * (3 * K * H + H * N)

F32 = mybir.dt.float32
BF16 = mybir.dt.bfloat16
I32 = mybir.dt.int32
U32 = mybir.dt.uint32
U16 = mybir.dt.uint16
U8 = mybir.dt.uint8
FP8X4 = mybir.dt.float8_e4m3fn_x4
FP4X4 = mybir.dt.float4_e2m1fn_x4
ADD = mybir.AluOpType.add
MULT = mybir.AluOpType.mult
IDENTITY = mybir.ActivationFunctionType.Identity

P = 128
HALF = 512
AHEAD = 2048


def tile_list_bilinear_flux_update_kernel(
    tc, tab_words, tab_scales, offs, wa, wb_words, wb_scales, wc_words, wc_scales, bb, wf, bf, out
):
    nc = tc.nc
    with ExitStack() as ctx:
        lists = ctx.enter_context(tc.tile_pool(name="lists", bufs=1))
        sb = ctx.enter_context(tc.tile_pool(name="sb", bufs=1))
        shared = ctx.enter_context(tc.tile_pool(name="shared", bufs=1))
        psum = ctx.enter_context(tc.psum_pool(name="psum", bufs=1))

        def tile(name, shape, dtype):
            return sb.tile(shape, dtype, name=name, align_bytes=256)

        def shifted(name, words):
            return tile(name, [P, words + 32], U32)[:, 32:]

        def placed(name, shape, dtype, kib):
            return shared.tile(shape, dtype, name=name, align_bytes=256, offset=1024 * kib)

        bank = [psum.tile([P, 512], F32, name=f"bank{i}") for i in range(8)]

        offsets = lists.tile([P, S // 16], U16, name="offsets")
        table = [placed("table0", [P, T], U32, 0), placed("table1", [P, T], U32, 16)]
        table_sc = placed("table_sc", [P, T], U8, 31)
        picked_sc = tile("picked_sc", [P, S], U8)
        v_sc = tile("v_sc", [P, 2 * S], U8)
        w_sc_raw = tile("w_sc_raw", [P, 2, H], U8)
        wb_raw = placed("wb_raw", [P, 2, 2 * H], U8, 50)
        wc_raw = placed("wc_raw", [P, 2, H], I32, 51)
        wa_raw = [placed(f"wa_raw{a}", [P, 4, H], F32, 34 + 9 * a) for a in range(2)]
        bias_rows = tile("bias_rows", [P, P], F32)
        identity = tile("identity", [P, P], F32)
        bias = tile("bias", [P, 8], F32)

        nc.vector.memset(table_sc[32:64, :].bitcast(I32), 0)
        nc.vector.memset(table_sc[64:P, :].bitcast(I32), 0)
        w_sc = tile("w_sc", [P, 2, H], U8)

        def load_words(a, t0, t1):
            words = tab_words[a].rearrange("p t i -> p (t i)").bitcast(I32)
            nc.sync.dma_start(out=table[a][:, t0:t1].bitcast(I32), in_=words[:, t0:t1])

        def load_w_scales(dst, src, row0):
            for q in range(4):
                nc.sync.dma_start(
                    out=dst[32 * q + row0 : 32 * q + row0 + 4, :, :].bitcast(I32),
                    in_=src[:, 4 * q : 4 * q + 4, :].rearrange("a r n -> r a n").bitcast(I32),
                )

        wa_rows = wa.rearrange("(a p j) c -> a p j c", a=2, j=4)
        nc.sync.dma_start(offsets[:], offs)
        nc.sync.dma_start(out=table_sc[0:32, :].bitcast(I32), in_=tab_scales.rearrange("a q t -> q a t").bitcast(I32))
        nc.sync.dma_start(out=wb_raw[:].bitcast(I32), in_=wb_words.rearrange("a p n -> p a n").bitcast(I32))
        load_w_scales(w_sc_raw, wb_scales, 0)
        load_words(0, 0, T)
        load_w_scales(w_sc_raw, wc_scales, 4)
        load_words(1, 0, AHEAD)

        nc.gpsimd.memset(bias_rows[:], 0.0)
        nc.gpsimd.dma_start(
            out=bias_rows[0:4, :].rearrange("t (g e) -> t g e", e=8), in_=bb.rearrange("(g t e) -> t g e", t=4, e=8)
        )
        nc.gpsimd.dma_start(out=bias_rows[4:8, :], in_=bf.rearrange("(t m) -> t m", t=4))
        make_identity(nc, identity[:])
        nc.gpsimd.memset(v_sc[:].bitcast(I32), 0)
        nc.gpsimd.memset(w_sc[:].bitcast(I32), 0)
        nc.tensor.transpose(bank[7][:, 0:P], bias_rows[:], identity[:])
        nc.scalar.copy(bias[:], bank[7][:, 0:8])

        v = [[tile(f"v{a}{h}", [P, HALF], U32) for h in range(2)] for a in range(2)]

        def gather_words(a, h):
            nc.vector.tensor_copy(v[a][h][:], table[a][:].indirect(offsets[:, 32 * h : 32 * (h + 1)]))

        def v_plane(a, cols):
            return v_sc[:, S * a + cols.start : S * a + cols.stop]

        nc.vector.tensor_copy(picked_sc[:], table_sc[:].indirect(offsets[:]))
        for q in (0, 2, 1, 3):
            nc.sync.dma_start(
                out=v_sc[32 * q : 32 * q + 4, :].bitcast(I32), in_=picked_sc[8 * q : 8 * q + 8, :].bitcast(I32)
            )
        load_words(1, AHEAD, T)
        nc.sync.dma_start(out=wa_raw[0][:], in_=wa_rows[0])

        wb_q = shifted("wb_q", H).bitcast(U8).rearrange("p (a n) -> p a n", a=2)
        wc_q = shifted("wc_q", 2 * H).rearrange("p (a n) -> p a n", a=2)

        def deal(engine, dst, src, words):
            engine.tensor_copy(
                dst.bitcast(I32).rearrange("p a (t g e) -> p a t g e", t=4, e=words),
                src.bitcast(I32).rearrange("p a (g t e) -> p a t g e", t=4, e=words),
            )

        deal(nc.vector, wb_q[:], wb_raw[:], 4)
        for q in range(4):
            deal(nc.gpsimd, w_sc[32 * q : 32 * q + 8], w_sc_raw[32 * q : 32 * q + 8], 2)
        nc.sync.dma_start(out=wa_raw[1][:], in_=wa_rows[1])
        nc.sync.dma_start(out=wc_raw[:], in_=wc_words.rearrange("a p n i -> p a (n i)").bitcast(I32))
        gather_words(0, 0)
        gather_words(0, 1)

        def b_pass(a, h, j):
            cols = slice(h * HALF, (h + 1) * HALF)
            nc.tensor.matmul_mx(
                out=bank[4 * h + j][:],
                lhsT=wb_q[:, a, 256 * j : 256 * (j + 1)].bitcast(FP4X4),
                lhsT_scale=w_sc[:, a, 128 * j : 128 * (j + 1)],
                rhs=v[a][h][:].bitcast(FP8X4),
                rhs_scale=v_plane(a, cols),
                start=(a == 0),
                stop=(a == 1),
            )

        for h in range(2):
            for j in range(4):
                b_pass(0, h, j)

        b_sb = [
            [tile(f"b_sb0{jj}", [P, 2, HALF], F32) for jj in range(2)],
            [placed(f"b_sb1{jj}", [P, 2, HALF], F32, 43 + 4 * jj) for jj in range(2)],
        ]

        def add_background(h, j):
            nc.scalar.activation(
                b_sb[h][j // 2][:, j % 2, :], bank[4 * h + j][:], IDENTITY, bias=bias[:, j : j + 1]
            )

        for h in range(2):
            gather_words(1, h)
            for j in range(4):
                b_pass(1, h, j)
        for j in range(4):
            add_background(0, j)

        wf_raw = placed("wf_raw", [P, 4, N], F32, 0)
        wf_rows = wf.rearrange("(g t e) n -> t g e n", t=4, e=8)
        for t in range(4):
            nc.sync.dma_start(out=wf_raw[:, t, :], in_=wf_rows[t])

        c_bank = (4, 5, 6, 0, 5, 6, 5, 6)
        a_bank = ((0, 1), (2, 3), (2, 4), (1, 3))

        def c_group(g):
            h, n0 = divmod(128 * g, HALF)
            for j in range(4):
                for a in range(2):
                    nc.tensor.matmul_mx(
                        out=bank[c_bank[g]][:, 128 * j : 128 * (j + 1)],
                        lhsT=wc_q[:, a, 128 * j : 128 * (j + 1)].bitcast(FP8X4),
                        lhsT_scale=w_sc[4:P, a, 128 * j : 128 * (j + 1)],
                        rhs=v[a][h][:, n0 : n0 + 128].bitcast(FP8X4),
                        rhs_scale=v_plane(a, slice(128 * g, 128 * (g + 1))),
                        start=(a == 0 and j == 0),
                        stop=(a == 1 and j == 3),
                    )

        wa_bf = [tile(f"wa_bf{a}", [P, 4 * H], BF16) for a in range(2)]
        wa_q = [shifted(f"wa_q{a}", H) for a in range(2)]
        wa_sc = [tile(f"wa_sc{a}", [P, H], U8) for a in range(2)]

        def a_pass(c, a, j):
            n0, n = 256 * c, 256
            h, m0 = divmod(n0, HALF)
            nc.tensor.matmul_mx(
                out=bank[a_bank[c][j // 2]][:, (j % 2) * 256 : (j % 2 + 1) * 256],
                lhsT=wa_q[a][:, 128 * j : 128 * (j + 1)].bitcast(FP8X4),
                lhsT_scale=wa_sc[a][:, 128 * j : 128 * (j + 1)],
                rhs=v[a][h][:, m0 : m0 + n].bitcast(FP8X4),
                rhs_scale=v_plane(a, slice(n0, n0 + n)),
                start=(a == 0 and j % 2 == 0),
                stop=(a == 1 and j % 2 == 1),
            )

        wa_dst = [wa_bf[a][:].rearrange("p (t g f e j) -> p t g f j e", t=4, f=2, e=4, j=4) for a in range(2)]
        wa_src = [wa_raw[a][:].rearrange("p j (g t f e) -> p t g f j e", t=4, f=2, e=4) for a in range(2)]

        def quantize_wa(a, j, tiles):
            nc.vector.quantize_mx(
                out=wa_q[a][:, 128 * j : 128 * (j + tiles)].bitcast(FP8X4),
                scales=wa_sc[a][:, 128 * j : 128 * (j + tiles)],
                in_=wa_bf[a][:, 512 * j : 512 * (j + tiles)],
            )

        for t in range(3):
            nc.vector.tensor_copy(wa_dst[0][:, t], wa_src[0][:, t])
        quantize_wa(0, 0, 2)
        nc.vector.tensor_copy(wa_dst[0][:, 3], wa_src[0][:, 3])
        quantize_wa(0, 2, 2)
        for jj in range(2):
            for c in range(2):
                for j in (2 * jj, 2 * jj + 1):
                    a_pass(c, 0, j)

        for t in range(2):
            nc.vector.tensor_copy(wa_dst[1][:, t], wa_src[1][:, t])
            nc.scalar.copy(wa_dst[1][:, 2 + t], wa_src[1][:, 2 + t])
        for j in range(2):
            add_background(1, j)
        quantize_wa(1, 0, 1)
        quantize_wa(1, 1, 1)
        deal(nc.vector, wc_q[:], wc_raw[:], 8)
        quantize_wa(1, 2, 1)
        quantize_wa(1, 3, 1)

        def a_pair(c, jj):
            for a in (1,) if c < 2 else (0, 1):
                for j in (2 * jj, 2 * jj + 1):
                    a_pass(c, a, j)

        ab = [tile(f"ab{c}", [P, 2, 256, 2], F32) for c in range(4)]

        def multiply_pair(c, jj, n0=0, n=256):
            cols = slice(256 * (c % 2) + n0, 256 * (c % 2) + n0 + n)
            nc.vector.tensor_tensor(
                ab[c][:, jj, n0 : n0 + n],
                bank[a_bank[c][jj]][:].rearrange("p (e n) -> p n e", e=2)[:, n0 : n0 + n],
                b_sb[c // 2][jj][:, :, cols].rearrange("p e n -> p n e"),
                MULT,
            )

        wf_bf = tile("wf_bf", [P, 4 * N], BF16)
        wf_q = shifted("wf_q", N)
        wf_sc = tile("wf_sc", [P, N], U8)
        wf_dst = wf_bf[:].rearrange("p (c i j) -> p c j i", i=4, j=4)
        wf_src = wf_raw[:].rearrange("p j (c i) -> p c j i", i=4)

        h_bf = tile("h_bf", [P, 4 * HALF], BF16)
        h_q = tile("h_q", [P, S], U32)
        h_sc = tile("h_sc", [P, S], U8)
        out_rows = out.rearrange("(t p) s -> p t s", p=P)

        def finish_h(g):
            n0 = 128 * (g % 2)
            nc.vector.tensor_tensor(
                h_bf[:, 512 * (g % 4) : 512 * (g % 4 + 1)].rearrange("p (n jj e) -> p n jj e", jj=2, e=2),
                bank[c_bank[g]][:].rearrange("p (jj e n) -> p n jj e", jj=2, e=2),
                ab[g // 2][:, :, n0 : n0 + 128, :].rearrange("p jj n e -> p n jj e"),
                ADD,
            )

        def quantize_h(n0, n):
            nc.vector.quantize_mx(
                out=h_q[:, n0 : n0 + n].bitcast(FP8X4),
                scales=h_sc[:, n0 : n0 + n],
                in_=h_bf[:, 4 * (n0 % HALF) : 4 * (n0 % HALF + n)],
            )

        def flux_pass(dst, t, n0, n):
            nc.tensor.matmul_mx(
                out=dst,
                lhsT=wf_q[:, 128 * t : 128 * (t + 1)].bitcast(FP8X4),
                lhsT_scale=wf_sc[:, 128 * t : 128 * (t + 1)],
                rhs=h_q[:, n0 : n0 + n].bitcast(FP8X4),
                rhs_scale=h_sc[:, n0 : n0 + n],
                start=True,
                stop=True,
            )

        def add_bias(dst, src, t, on_vector):
            if on_vector:
                nc.vector.tensor_scalar(dst, src, bias[:, 4 + t : 5 + t], None, ADD)
            else:
                nc.scalar.activation(dst, src, IDENTITY, bias=bias[:, 4 + t : 5 + t])

        results = {}

        def flux(n0, n, banks):
            y = tile(f"y{n0}", [P, 4, n], F32)
            place = [len([b for b in banks[:t] if b == banks[t]]) for t in range(4)]
            sums = [bank[banks[t]][:, place[t] * n : (place[t] + 1) * n] for t in range(4)]
            for t in range(4):
                flux_pass(sums[t], t, n0, n)
            results[n0] = (n, y, sums)

        def finish_rows(n0, tiles, on_vector=False):
            n, y, sums = results[n0]
            for t in tiles:
                add_bias(y[:, t, :], sums[t], t, on_vector)

        def store(n0, t0, t1):
            n, y, sums = results[n0]
            nc.sync.dma_start(out=out_rows[:, t0:t1, n0 : n0 + n], in_=y[:, t0:t1, :])

        c_sb = {g: tile(f"c_sb{g}", [P, 2, 128, 2], F32) for g in (0, 4)}

        def copy_c(g):
            nc.scalar.copy(c_sb[g][:], bank[c_bank[g]][:].rearrange("p (jj e n) -> p jj n e", jj=2, e=2))

        def finish_on_gpsimd(g, jj):
            nc.gpsimd.tensor_tensor(
                h_bf[:, 0:512].rearrange("p (n jj e) -> p jj n e", jj=2, e=2)[:, jj],
                ab[g // 2][:, jj, 0:128],
                c_sb[g][:, jj],
                ADD,
            )

        for jj in range(2):
            for c in range(2):
                a_pair(c, jj)
        c_group(0)
        copy_c(0)
        for s in range(2):
            nc.scalar.copy(wf_dst[:, 64 * s : 64 * (s + 1)], wf_src[:, 64 * s : 64 * (s + 1)])
        for j in range(2, 4):
            add_background(1, j)
        c_group(1)
        c_group(2)
        multiply_pair(0, 0)
        finish_on_gpsimd(0, 0)
        c_group(3)
        multiply_pair(1, 0)
        multiply_pair(0, 1)
        finish_on_gpsimd(0, 1)
        multiply_pair(1, 1)
        for jj in range(2):
            a_pair(2, jj)
        finish_h(1)
        c_group(4)
        copy_c(4)
        finish_h(2)
        c_group(5)
        finish_h(3)
        a_pair(3, 0)
        multiply_pair(2, 0)
        nc.vector.quantize_mx(out=wf_q[:].bitcast(FP8X4), scales=wf_sc[:], in_=wf_bf[:])
        quantize_h(0, 512)
        finish_on_gpsimd(4, 0)
        multiply_pair(2, 1)
        finish_on_gpsimd(4, 1)
        flux(0, 512, (0, 2, 7, 4))
        for t0, t1 in ((0, 1), (1, 2), (2, 4)):
            finish_rows(0, range(t0, t1))
            store(0, t0, t1)
        a_pair(3, 1)
        c_group(6)
        multiply_pair(3, 0)
        finish_h(5)
        c_group(7)
        multiply_pair(3, 1, 0, 128)
        quantize_h(512, 256)
        flux(512, 256, (1, 1, 0, 4))
        finish_rows(512, (0, 1))
        store(512, 0, 2)
        finish_rows(512, (2,))
        finish_h(6)
        multiply_pair(3, 1, 128, 128)
        quantize_h(768, 128)
        finish_h(7)
        finish_rows(512, (3,), True)
        store(512, 2, 4)
        quantize_h(896, 128)
        flux(768, 128, (2, 2, 3, 3))
        finish_rows(768, (0, 1))
        finish_rows(768, (2, 3), True)
        store(768, 0, 4)
        flux(896, 128, (5, 5, 7, 7))
        finish_rows(896, (0, 1))
        finish_rows(896, (2, 3), True)
        store(896, 0, 4)
